import numpy as np
import ml_dtypes


def mxq(x, axis, fmt="e4m3"):
    dtype, down = {"e4m3": (ml_dtypes.float8_e4m3fn, 7), "e5m2": (ml_dtypes.float8_e5m2, 14)}[fmt]
    v = np.moveaxis(np.asarray(x, np.float32).astype(ml_dtypes.bfloat16).astype(np.float64), axis, -1)
    blocks = v.reshape(v.shape[:-1] + (-1, 32))
    amax = np.abs(blocks).max(-1, keepdims=True)
    byte = np.maximum(np.where(amax > 0, np.frexp(amax)[1] - 1 + 127, 0) - down, 1)
    scale = np.exp2(byte - 127.0)
    codes = (blocks / scale).astype(np.float32).astype(dtype).astype(np.float64)
    return np.moveaxis((codes * scale).reshape(v.shape), -1, axis)


WIDE = False


def mx_kscale(k):
    if not WIDE:
        return np.ones(k)
    levels = np.array([10, -10, 5, -5, 0])
    if k % 512:
        return np.exp2(np.random.permutation(np.resize(levels, k // 32))).repeat(32)
    a = np.empty((k // 512, 16))
    for p in range(k // 512):
        a[p, :8] = np.random.permutation(np.resize(levels, 8))
        for g in range(8):
            far = levels[np.abs(levels - a[p, g]) >= 10]
            a[p, g + 8] = far[np.random.randint(len(far))]
    return np.exp2(a.ravel()).repeat(32)


def f64(x):
    return np.asarray(x).astype(np.float64)


def striped(idx):
    return np.tile(idx.reshape(-1, 16).T, (8, 1)).astype(np.uint16)


def unstriped(offs):
    return offs[:16].T.reshape(-1).astype(np.int64)


E2M1 = np.array([0.0, 0.5, 1.0, 1.5, 2.0, 3.0, 4.0, 6.0, -0.0, -0.5, -1.0, -1.5, -2.0, -3.0, -4.0, -6.0])


def pack_weight(w, fmt):
    k, n = w.shape
    w = f64(np.asarray(w, np.float32).astype(ml_dtypes.bfloat16)).reshape(k // 32, 32, n)
    amax = np.abs(w).max(1)
    if fmt == "e4m3":
        byte = np.frexp(amax)[1] - 1 + 127 - 7
    else:
        mant, ex = np.frexp(amax / 6.0)
        byte = np.where(mant > 0.5, ex, ex - 1) + 127
    byte = np.clip(np.where(amax > 0, byte, 1), 1, 254)
    scaled = (w * np.exp2(127.0 - byte)[:, None, :]).reshape(k, n).astype(np.float32)
    by_word = np.ascontiguousarray(scaled.reshape(k // 512, 128, 4, n).transpose(0, 1, 3, 2))
    if fmt == "e4m3":
        words = by_word.astype(ml_dtypes.float8_e4m3fn).view(np.uint8)
    else:
        c = by_word.astype(ml_dtypes.float4_e2m1fn).view(np.uint8) & 0xF
        words = (c[..., 0::2] | (c[..., 1::2] << 4)).reshape(k // 512, 128, 2 * n)
    return np.ascontiguousarray(words), np.ascontiguousarray(byte.astype(np.uint8).reshape(k // 512, 16, n))


def unpack_weight(words, scales, fmt):
    g, _, n = scales.shape
    words = np.ascontiguousarray(words).reshape(g, 128, n, -1)
    if fmt == "e4m3":
        vals = words.view(ml_dtypes.float8_e4m3fn).astype(np.float64)
    else:
        nib = np.empty((g, 128, n, 4), np.uint8)
        nib[..., 0::2] = words & 0xF
        nib[..., 1::2] = words >> 4
        vals = E2M1[nib]
    vals = vals * np.repeat(np.exp2(scales.astype(np.float64) - 127.0), 8, axis=1)[..., None]
    return vals.transpose(0, 1, 3, 2).reshape(g * 512, n)


def gelu(v):
    return 0.5 * v * (1.0 + np.tanh(np.sqrt(2.0 / np.pi) * (v + 0.044715 * v**3)))


def bf(x):
    return np.asarray(x, np.float32).astype(ml_dtypes.bfloat16)


def planes(Y):
    n, m = Y.shape
    b = f64(bf(Y)).reshape(n // 32, 32, m)
    amax = np.abs(b).max(1)
    byte = np.clip(np.where(amax > 0, np.frexp(amax)[1] - 1 + 127 - 7, 1), 1, 254)
    codes = (b * np.exp2(127.0 - byte)[:, None, :]).reshape(n, m).astype(np.float32).astype(ml_dtypes.float8_e4m3fn).view(np.uint8)
    words = codes.reshape(n // 512, 128, 4, m).transpose(0, 1, 3, 2)
    return np.ascontiguousarray(words), np.ascontiguousarray(byte.astype(np.uint8).reshape(n // 512, 16, m))


K, T, S, T2, H, M, N = 512, 2048, 512, 1024, 1024, 512, 512

def setup_inputs():
    n = np.random.standard_normal
    s, u, d = mx_kscale(K)[:, None], mx_kscale(H)[:, None], mx_kscale(M)[:, None]
    gain = np.exp(0.8 * n((1, N)))
    tab_words, tab_scales = pack_weight(n((K, T)) * s, "e4m3")
    w2_words, w2_scales = pack_weight(1.5 * n((K, H)) / s / np.sqrt(K), "e2m1")
    w3_words, w3_scales = pack_weight(n((K, H)) / s * u.T / np.sqrt(K), "e4m3")
    w5_words, w5_scales = pack_weight(n((H, N)) / u * gain / np.sqrt(H), "e2m1")
    return {
        "tab_words": tab_words, "tab_scales": tab_scales,
        "offs": striped(np.random.permutation(T)[:S]),
        "offs2": striped(np.random.permutation(T2)[:S]),
        "offs3": striped(np.random.permutation(T2)[:S]),
        "w1": (1.5 * n((K, H)) / s / np.sqrt(K)).astype(np.float32),
        "w2_words": w2_words, "w2_scales": w2_scales,
        "w3_words": w3_words, "w3_scales": w3_scales,
        "w4": (n((K, H)) / s / np.sqrt(K)).astype(np.float32),
        "wg1": np.exp(0.3 * n((128, S))).astype(np.float32),
        "wg2": np.exp(0.3 * n((128, S))).astype(np.float32),
        "level": (1.5 * n((H, T2)) * u).astype(np.float32),
        "w5_words": w5_words, "w5_scales": w5_scales,
        "cells": (n((M, T2)) * d).astype(np.float32),
        "w6": (0.7 * n((M, N)) / d * gain / np.sqrt(M)).astype(np.float32),
    }

def reference(tab_words, tab_scales, offs, offs2, offs3, w1, w2_words, w2_scales, w3_words, w3_scales,
              w4, wg1, wg2, level, w5_words, w5_scales, cells, w6):
    v = unpack_weight(tab_words, tab_scales, "e4m3")[:, unstriped(offs)]
    h1 = np.maximum(mxq(f64(w1), 0, "e4m3").T @ v,
                    unpack_weight(w2_words, w2_scales, "e2m1").T @ v)
    h2 = (unpack_weight(w3_words, w3_scales, "e4m3").T @ v) * np.tanh(
        mxq(f64(w4), 0, "e4m3").T @ v)
    pageA = np.zeros((H, T2))
    pageA[:, unstriped(offs2)] = np.tile(f64(wg1), (H // 128, 1)) * h1
    pageB = np.zeros((H, T2))
    pageB[:, unstriped(offs3)] = np.tile(f64(wg2), (H // 128, 1)) * h2
    z = f64(level) * (1.0 / (1.0 + np.exp(-pageA))) + pageB
    y = (unpack_weight(w5_words, w5_scales, "e2m1").T @ mxq(z, 0, "e4m3")
              + mxq(f64(w6), 0, "e4m3").T @ mxq(f64(cells), 0, "e4m3"))
    words, scales = planes(y)
    return y, words, scales

@@ -1,0 +1,398 @@
+from contextlib import ExitStack
+
+import concourse.mybir as mybir
+from concourse.masks import make_identity
+
+K, T, S, T2, H, M, N = 512, 2048, 512, 1024, 1024, 512, 512
+FLOPS = 2 * (4 * K * H * S + (H + M) * N * T2)
+
+F32 = mybir.dt.float32
+BF16 = mybir.dt.bfloat16
+I32 = mybir.dt.int32
+U32 = mybir.dt.uint32
+U16 = mybir.dt.uint16
+U8 = mybir.dt.uint8
+E4M3 = mybir.dt.float8_e4m3fn_x4
+E2M1 = mybir.dt.float4_e2m1fn_x4
+ALU = mybir.AluOpType
+ACT = mybir.ActivationFunctionType
+
+P = 128
+PACK = 4
+SLICES = H // P
+HALF = 512
+W1_CUTS = (0, 128, 384, 640, 896, 1024)
+W4_CUTS = (0, 256, 512, 768, 1024)
+GP = 1
+PA = 2
+PB = 2
+GATE = 2
+GATED = 1
+AHEAD = 5
+ORDER = 0
+S_W6 = 2
+S_CELLS = 4
+S_DEAL = 0
+GRP = 3
+PLQ = 0
+WARM = 1
+PREP_POS = 0
+SRC = 2
+SNK = 1
+
+
+def tile_list_manhole_source_sink_kernel(
+    tc, tab_words, tab_scales, offs, offs2, offs3, w1, w2_words, w2_scales, w3_words, w3_scales,
+    w4, wg1, wg2, level, w5_words, w5_scales, cells, w6, out_0, out_1, out_2,
+):
+    nc = tc.nc
+    with ExitStack() as ctx:
+        keep = ctx.enter_context(tc.tile_pool(name="keep", bufs=1))
+        ring = ctx.enter_context(tc.tile_pool(name="ring", bufs=2))
+        psum = ctx.enter_context(tc.psum_pool(name="psum", bufs=1))
+
+        def held(name, shape, dtype, tag=""):
+            return keep.tile(shape, dtype, name=name, tag=tag or name, align_bytes=64)
+
+        def bank(b):
+            return psum.tile([P, HALF], F32, name="bank%d" % b)
+
+        def load(tile_ap, dram_ap):
+            nc.sync.dma_start(out=tile_ap, in_=dram_ap)
+
+        def load_plane(queue, plane, scales):
+            for q in range(4):
+                queue.dma_start(
+                    out=plane[32 * q : 32 * q + 4].bitcast(I32),
+                    in_=scales[:, 4 * q : 4 * q + 4, :].rearrange("a r c -> r a c").bitcast(I32),
+                )
+
+        def zero_plane(name, passes, width):
+            plane = held(name, [P, passes, width], U8)
+            nc.vector.memset(plane[:].rearrange("p a c -> p (a c)").bitcast(I32), 0)
+            return plane
+
+        def load_rows(name, rows):
+            raw = held(name, [P, PACK, rows.shape[1]], F32)
+            load(raw[:], rows.rearrange("(p i) c -> p i c", i=PACK))
+            return raw
+
+        def round_rows(raw, grouped, c0, c1):
+            nc.scalar.copy(
+                out=grouped[:, PACK * c0 : PACK * c1].rearrange("p (c j i) -> p c i j", j=4, i=PACK),
+                in_=raw[:, :, c0:c1].rearrange("p i (c j) -> p c i j", j=4),
+            )
+
+        def quantize(name, grouped, width):
+            codes = held(name + "_codes", [P, width], U32)
+            scales = held(name + "_scales", [P, width], U8)
+            nc.vector.quantize_mx(out=codes[:].bitcast(E4M3), scales=scales[:], in_=grouped[:])
+            return codes, scales
+
+        def mx(out, lhs, rhs, start=True, stop=True):
+            nc.tensor.matmul_mx(
+                out=out, lhsT=lhs[0], lhsT_scale=lhs[1], rhs=rhs[0], rhs_scale=rhs[1], start=start, stop=stop
+            )
+
+        tab_plane = held("tab_plane", [P, T], U8)
+        nc.vector.memset(tab_plane[:].bitcast(I32), 0)
+        w2_plane = zero_plane("w2_plane", 1, H)
+        w3_plane = zero_plane("w3_plane", 1, H)
+        w5_plane = zero_plane("w5_plane", 2, N)
+        pages_a = [held("page_a%d" % k, [P, T2], F32) for k in range(PA)]
+        pages_b = [held("page_b%d" % k, [P, T2], F32) for k in range(PB)]
+        for page in pages_a + pages_b:
+            nc.vector.memset(page[:], 0.0)
+        if PLQ:
+            load_plane(nc.gpsimd, w2_plane, w2_scales)
+            load_plane(nc.gpsimd, w3_plane, w3_scales)
+        if WARM:
+            warm = held("warm", [P, 8], F32)
+            nc.scalar.activation(out=warm[:], in_=pages_a[0][:, 0:8], func=ACT.Sigmoid)
+        ident = held("ident", [P, P], F32)
+        make_identity(nc, ident[:])
+
+        list1 = held("list1", [P, S // 16], U16)
+        list2 = held("list2", [P, S // 16], U16)
+        list3 = held("list3", [P, S // 16], U16)
+        tab = held("tab", [P, T], U32)
+        w2 = held("w2", [P, 2 * H], U8)
+        w3 = held("w3", [P, H], U32)
+        w5 = held("w5", [P, 2, 2 * N], U8)
+        gain1 = held("gain1", [P, S], F32)
+        gain2 = held("gain2", [P, S], F32)
+        w1_raw, w4_raw, level_sb = [], [], []
+
+        def load_w1(c):
+            w1_raw.append(load_rows("w1_raw%d" % c, w1[:, W1_CUTS[c] : W1_CUTS[c + 1]]))
+
+        def load_w4(c):
+            w4_raw.append(load_rows("w4_raw%d" % c, w4[:, W4_CUTS[c] : W4_CUTS[c + 1]]))
+
+        def load_level(s):
+            rows = held("level%d" % s, [P, T2], F32)
+            load(rows[:], level[P * s : P * (s + 1), :])
+            level_sb.append(rows)
+
+        load(tab[:].bitcast(I32), tab_words[0].rearrange("p t i -> p (t i)").bitcast(I32))
+        nc.sync.dma_start(list1[:], offs)
+        for q in range(4):
+            load(tab_plane[32 * q : 32 * q + 4, :].bitcast(I32), tab_scales[0, 4 * q : 4 * q + 4, :].bitcast(I32))
+        load_w1(0)
+        load(w2[:].bitcast(I32), w2_words[0].bitcast(I32))
+        if not PLQ:
+            load_plane(nc.sync, w2_plane, w2_scales)
+        nc.sync.dma_start(list2[:], offs2)
+        load(gain1[:], wg1)
+        load_w4(0)
+        load(w3[:].bitcast(I32), w3_words[0].rearrange("p c i -> p (c i)").bitcast(I32))
+        if not PLQ:
+            load_plane(nc.sync, w3_plane, w3_scales)
+        load_w1(1)
+        load(gain2[:], wg2)
+        load_level(0)
+        nc.sync.dma_start(list3[:], offs3)
+        cells_raw = []
+
+        def load_w5():
+            load(w5[:].bitcast(I32), w5_words.rearrange("a p c -> p a c").bitcast(I32))
+            load_plane(nc.sync, w5_plane, w5_scales)
+
+        def load_cells(h):
+            cells_raw.append(load_rows("cells_raw%d" % h, cells[:, HALF * h : HALF * (h + 1)]))
+
+        w6_raw = held("w6_raw", [P, PACK, N], F32)
+        jobs = {"a": load_w1, "b": load_w4, "l": load_level, "c": load_cells, "f": lambda k: load_w5(),
+                "s": lambda k: load(w6_raw[:], w6.rearrange("(p i) c -> p i c", i=PACK))}
+        orders = (
+            "l1 b1 a2 l2 b2 a3 l3 b3 a4 l4 f0 s0 c0 c1 l5 l6 l7",
+            "b1 a2 b2 a3 b3 a4 l1 l2 f0 s0 l3 c0 c1 l4 l5 l6 l7",
+            "b1 a2 l1 b2 a3 b3 a4 l2 f0 s0 c0 c1 l3 l4 l5 l6 l7",
+            "b1 a2 b2 a3 b3 a4 f0 l1 s0 c0 l2 c1 l3 l4 l5 l6 l7",
+            "b1 a2 l1 b2 a3 l2 b3 a4 f0 l3 s0 l4 c0 l5 c1 l6 l7",
+        )
+        for job in orders[ORDER].split():
+            jobs[job[0]](int(job[1]))
+
+        v_codes = held("v_codes", [P, S], U32)
+        v_scales = held("v_scales", [P, S], U8)
+        nc.vector.tensor_copy(v_codes[:], tab[:].indirect(list1[:]))
+        nc.vector.tensor_copy(v_scales[:], tab_plane[:].indirect(list1[:]))
+        v = (v_codes[:].bitcast(E4M3), v_scales[:])
+
+        w1_q, w4_q = {}, {}
+
+        def prepare(name, raw, cuts, c, table):
+            width = cuts[c + 1] - cuts[c]
+            grouped = ring.tile([P, PACK * width], BF16, name="grouped", align_bytes=64, bufs=GRP)
+            round_rows(raw[c], grouped, 0, width)
+            codes, scales = quantize("%s_%d" % (name, c), grouped, width)
+            for s in range(cuts[c] // P, cuts[c + 1] // P):
+                cols = slice(P * s - cuts[c], P * (s + 1) - cuts[c])
+                table[s] = (codes[:, cols].bitcast(E4M3), scales[:, cols])
+
+        def source_products(s):
+            first, second = bank(0), bank(1)
+            mx(second[:], (w2[:, 2 * P * s : 2 * P * (s + 1)].bitcast(E2M1), w2_plane[:, 0, P * s : P * (s + 1)]), v)
+            mx(first[:], w1_q[s], v)
+            second_sb = ring.tile([P, S], F32, name="second_sb")
+            nc.scalar.copy(out=second_sb[:], in_=second[:])
+            return first, second_sb
+
+        def sink_products(s):
+            third, fourth = bank(2), bank(3)
+            mx(fourth[:], w4_q[s], v)
+            mx(third[:], (w3[:, P * s : P * (s + 1)].bitcast(E4M3), w3_plane[:, 0, P * s : P * (s + 1)]), v)
+            squashed = ring.tile([P, S], F32, name="squashed")
+            nc.scalar.activation(out=squashed[:], in_=fourth[:], func=ACT.Tanh)
+            if not GP:
+                return third, squashed
+            weighted = ring.tile([P, S], F32, name="weighted")
+            nc.gpsimd.tensor_tensor(out=weighted[:], in0=squashed[:], in1=gain2[:], op=ALU.mult)
+            return third, weighted
+
+        def combine(slot, pair, op):
+            h = ring.tile([P, S], F32, name=slot, bufs=SRC if slot == "sources" else SNK, align_bytes=64)
+            nc.vector.tensor_tensor(out=h[:], in0=pair[0][:], in1=pair[1][:], op=op)
+            return h
+
+        def turn_into(sums, rows, first):
+            for b in range(T2 // P):
+                nc.tensor.matmul(
+                    sums[b // 4][:, P * (b % 4) : P * (b % 4 + 1)],
+                    lhsT=rows[:, P * b : P * (b + 1)],
+                    rhs=ident[:],
+                    is_transpose=True,
+                    start=first and b % 4 == 0,
+                    stop=(not first) and b % 4 == 3,
+                )
+
+        z_turned = {}
+
+        def round_z(s, h, sums, copy):
+            if s % 4 == 0:
+                z_turned[s // 4, h] = held("z_turned%d" % h, [P, 4 * HALF], BF16)
+            copy(
+                out=z_turned[s // 4, h][:].rearrange("t (u b s q e) -> t u b s q e", u=2, b=4, s=4, e=2)[
+                    :, :, :, s % 4, :, :
+                ],
+                in_=sums[:].rearrange("t (b q u e) -> t u b q e", b=4, u=2, e=2),
+            )
+
+        def turn_back(a, h, banks, copies):
+            words = z_turned[a, h][:].bitcast(F32)
+            grouped = ring.tile([P, PACK * HALF], BF16, name="z_grouped", align_bytes=64)
+            for k in range(2):
+                turned = bank(banks[k])
+                for u in range(2):
+                    for bb in range(2):
+                        src = (4 * u + 2 * k + bb) * P
+                        dst = (2 * u + bb) * P
+                        nc.tensor.transpose(turned[:, dst : dst + P], words[:, src : src + P], ident[:])
+                copies[k](
+                    out=grouped[:].bitcast(F32)[:, HALF * k : HALF * (k + 1)].rearrange("p (c u) -> p c u", u=2),
+                    in_=turned[:].rearrange("p (u c) -> p c u", u=2),
+                )
+            codes, scales = quantize("z%d%d" % (a, h), grouped, HALF)
+            return codes[:].bitcast(E4M3), scales[:]
+
+        w5_dealt = {}
+        w5_plane_dealt = held("w5_plane_dealt", [P, 2, PACK, P], U8)
+
+        def deal_w5(a, tag):
+            w5_dealt[a] = ring.tile([P, PACK, 2 * P], U8, name="w5_dealt%d" % a, tag=tag, bufs=SNK, align_bytes=64)
+            nc.vector.tensor_copy(
+                out=w5_dealt[a][:].bitcast(U16),
+                in_=w5[:, a, :].bitcast(U16).rearrange("p (m t) -> p t m", t=PACK),
+            )
+
+        def prepare_w6():
+            grouped = held("w6_grouped", [P, PACK * N], BF16)
+            for k in range(2):
+                nc.scalar.copy(
+                    out=grouped[:].rearrange("p (t m i) -> p m i t", t=PACK, i=PACK)[:, 64 * k : 64 * (k + 1)],
+                    in_=w6_raw[:].rearrange("p i (m t) -> p m i t", t=PACK)[:, 64 * k : 64 * (k + 1)],
+                )
+            return quantize("w6", grouped, N)
+
+        def prepare_cells(h):
+            grouped = held("cells_grouped%d" % h, [P, PACK * HALF], BF16)
+            for k in range(2):
+                round_rows(cells_raw[h], grouped, 256 * k, 256 * (k + 1))
+            codes, scales = quantize("cells%d" % h, grouped, HALF)
+            return codes[:].bitcast(E4M3), scales[:]
+
+        def w5_slice(a, t):
+            return w5_dealt[a][:, t, :].bitcast(E2M1), w5_plane_dealt[:, a, t, :]
+
+        z_q, cells_q = {}, {}
+
+        def prepare_ahead(s):
+            if P * s in W1_CUTS[:-1]:
+                prepare("w1", w1_raw, W1_CUTS, W1_CUTS.index(P * s), w1_q)
+            if P * (s - 1) in W4_CUTS[:-1]:
+                prepare("w4", w4_raw, W4_CUTS, W4_CUTS.index(P * (s - 1)), w4_q)
+
+        prepare_ahead(0)
+        sources = combine("sources", source_products(0), ALU.max)
+        prepare_ahead(1)
+        source_pair = source_products(1)
+        sink_pair = sink_products(0)
+        sums = None
+
+        def prep(s):
+            for k in range(2 if s == 0 else s + AHEAD, s + AHEAD + 1):
+                prepare_ahead(k)
+
+        def scatter_sinks(s):
+            if GP:
+                nc.vector.tensor_copy(pages_b[s % PB][:].indirect(list3[:]), sinks[:])
+            else:
+                nc.vector.tensor_tensor(pages_b[s % PB][:].indirect(list3[:]), sinks[:], gain2[:], ALU.mult)
+
+        for s in range(SLICES):
+            page_a = pages_a[s % PA]
+            if PREP_POS == 0:
+                prep(s)
+            nc.vector.tensor_tensor(page_a[:].indirect(list2[:]), sources[:], gain1[:], ALU.mult)
+            if s + 1 < SLICES:
+                sources = combine("sources", source_pair, ALU.max)
+            if PREP_POS == 1:
+                prep(s)
+            if s + 2 < SLICES:
+                source_pair = source_products(s + 2)
+            gate = ring.tile([P, T2], F32, name="gate", bufs=GATE)
+            nc.scalar.activation(out=gate[:], in_=page_a[:], func=ACT.Sigmoid)
+            if s > 0:
+                scatter_sinks(s - 1)
+            sinks = combine("sinks", sink_pair, ALU.mult)
+            if s + 1 < SLICES:
+                sink_pair = sink_products(s + 1)
+            gated = ring.tile([P, T2], F32, name="gated", bufs=GATED)
+            (nc.gpsimd if GP else nc.vector).tensor_tensor(out=gated[:], in0=level_sb[s][:], in1=gate[:], op=ALU.mult)
+            if s > 0:
+                turn_into(sums, pages_b[(s - 1) % PB], False)
+                for h in range(2):
+                    round_z(s - 1, h, sums[h], nc.scalar.copy)
+            sums = [bank(4), bank(5)]
+            turn_into(sums, gated, True)
+            if s == S_DEAL:
+                deal_w5(0, "w5_dealt0")
+                nc.vector.tensor_copy(
+                    out=w5_plane_dealt[:], in_=w5_plane[:].rearrange("p a (m t) -> p a t m", t=PACK)
+                )
+            if s == S_W6:
+                w6_codes, w6_scales = prepare_w6()
+            if s == 4:
+                for h in range(2):
+                    z_q[0, h] = turn_back(0, h, (6, 7), (nc.scalar.copy, nc.scalar.copy))
+            if s in (S_CELLS, S_CELLS + 1):
+                cells_q[s - S_CELLS] = prepare_cells(s - S_CELLS)
+
+        def open_sum(t, h, b):
+            acc = bank(b)
+            cols = slice(P * t, P * (t + 1))
+            mx(acc[:], (w6_codes[:, cols].bitcast(E4M3), w6_scales[:, cols]), cells_q[h], True, False)
+            mx(acc[:], w5_slice(0, t), z_q[0, h], False, False)
+            return acc
+
+        scatter_sinks(SLICES - 1)
+        page_b = pages_b[(SLICES - 1) % PB]
+        deal_w5(1, "sinks")
+        accs = {(t, 0): open_sum(t, 0, t) for t in range(PACK)}
+        turn_into(sums, page_b, False)
+        round_z(SLICES - 1, 0, sums[0], nc.scalar.copy)
+        round_z(SLICES - 1, 1, sums[1], nc.vector.tensor_copy)
+        z_q[1, 0] = turn_back(1, 0, (6, 7), (nc.scalar.copy, nc.vector.tensor_copy))
+        z_q[1, 1] = turn_back(1, 1, (4, 5), (nc.scalar.copy, nc.scalar.copy))
+        for t in range(2):
+            accs[t, 1] = open_sum(t, 1, 6 + t)
+
+        y_rows = out_0.rearrange("(p t) c -> p t c", t=PACK)
+        y_words = out_1[0].rearrange("p c t -> p (c t)").bitcast(I32)
+        y_plane = held("y_plane", [P, T2], U8)
+        for h in range(2):
+            cols = slice(HALF * h, HALF * (h + 1))
+            if h == 1:
+                for t in range(2, PACK):
+                    accs[t, 1] = open_sum(t, 1, 2 + t)
+            y = held("y%d" % h, [P, PACK, HALF], F32, tag="cells_raw%d" % h)
+            for t in range(PACK):
+                mx(accs[t, h][:], w5_slice(1, t), z_q[1, h], False, True)
+                copy = nc.vector.tensor_copy if (t, h) == (1, 0) else nc.scalar.copy
+                copy(out=y[:, t, :], in_=accs[t, h][:])
+                if t % 2 == 1:
+                    nc.sync.dma_start(out=y_rows[:, t - 1 : t + 1, cols], in_=y[:, t - 1 : t + 1, :])
+            grouped = held("y_grouped%d" % h, [P, PACK * HALF], BF16, tag="cells_grouped%d" % h)
+            nc.vector.tensor_copy(
+                out=grouped[:].rearrange("p (c j t) -> p c t j", j=4, t=PACK),
+                in_=y[:].rearrange("p t (c j) -> p c t j", j=4),
+            )
+            y_codes = held("y_codes%d" % h, [P, HALF], U32)
+            nc.vector.quantize_mx(out=y_codes[:].bitcast(E4M3), scales=y_plane[:, cols], in_=grouped[:])
+            nc.sync.dma_start(out=y_words[:, cols], in_=y_codes[:].bitcast(I32))
+        for q in range(4):
+            queue = nc.sync if q % 2 == 0 else nc.scalar
+            queue.dma_start(
+                out=out_2[0, 4 * q : 4 * q + 4, :].bitcast(I32), in_=y_plane[32 * q : 32 * q + 4, :].bitcast(I32)
+            )

@@ -21,24 +21,33 @@ P = 128
 PACK = 4
 SLICES = H // P
 HALF = 512
-W1_CUTS = (0, 128, 384, 640, 896, 1024)
+W1_CUTS = (0, 256, 512, 768, 1024)
 W4_CUTS = (0, 256, 512, 768, 1024)
-GP = 1
+GP = 0
 PA = 2
-PB = 2
+PB = 1
 GATE = 2
-GATED = 1
-AHEAD = 5
-ORDER = 0
-S_W6 = 2
-S_CELLS = 4
-S_DEAL = 0
+GATED = 2
+AHEAD = 4
+ORDER = 3
+S_W6 = 5
+S_CELLS = 3
+S_DEAL = 5
 GRP = 3
-PLQ = 0
+PLQ = 1
 WARM = 1
 PREP_POS = 0
 SRC = 2
-SNK = 1
+SNK = 2
+TQ = 1
+W5E = 0
+LVL = 1
+RZ = 1
+STG = 1
+SPLIT0 = 1
+WC = 0
+VMASK = 10
+Y_CUTS = ((0, 512), (0, 512))
 
 
 def tile_list_manhole_source_sink_kernel(
@@ -67,9 +76,9 @@ def tile_list_manhole_source_sink_kernel(
                     in_=scales[:, 4 * q : 4 * q + 4, :].rearrange("a r c -> r a c").bitcast(I32),
                 )
 
-        def zero_plane(name, passes, width):
+        def zero_plane(engine, name, passes, width):
             plane = held(name, [P, passes, width], U8)
-            nc.vector.memset(plane[:].rearrange("p a c -> p (a c)").bitcast(I32), 0)
+            engine.memset(plane[:].rearrange("p a c -> p (a c)").bitcast(I32), 0)
             return plane
 
         def load_rows(name, rows):
@@ -83,9 +92,10 @@ def tile_list_manhole_source_sink_kernel(
                 in_=raw[:, :, c0:c1].rearrange("p i (c j) -> p c i j", j=4),
             )
 
-        def quantize(name, grouped, width):
+        def quantize(name, grouped, width, scales=None):
             codes = held(name + "_codes", [P, width], U32)
-            scales = held(name + "_scales", [P, width], U8)
+            if scales is None:
+                scales = held(name + "_scales", [P, width], U8)
             nc.vector.quantize_mx(out=codes[:].bitcast(E4M3), scales=scales[:], in_=grouped[:])
             return codes, scales
 
@@ -95,21 +105,17 @@ def tile_list_manhole_source_sink_kernel(
             )
 
         tab_plane = held("tab_plane", [P, T], U8)
-        nc.vector.memset(tab_plane[:].bitcast(I32), 0)
-        w2_plane = zero_plane("w2_plane", 1, H)
-        w3_plane = zero_plane("w3_plane", 1, H)
-        w5_plane = zero_plane("w5_plane", 2, N)
+        (nc.vector if PLQ else nc.gpsimd).memset(tab_plane[:].bitcast(I32), 0)
+        w2_plane = zero_plane(nc.gpsimd if PLQ else nc.vector, "w2_plane", 1, H)
+        w5_plane = zero_plane(nc.vector, "w5_plane", 2, N)
+        w3_plane = zero_plane(nc.vector, "w3_plane", 1, H)
         pages_a = [held("page_a%d" % k, [P, T2], F32) for k in range(PA)]
         pages_b = [held("page_b%d" % k, [P, T2], F32) for k in range(PB)]
         for page in pages_a + pages_b:
             nc.vector.memset(page[:], 0.0)
+        ident = held("ident", [P, P], F32)
         if PLQ:
             load_plane(nc.gpsimd, w2_plane, w2_scales)
-            load_plane(nc.gpsimd, w3_plane, w3_scales)
-        if WARM:
-            warm = held("warm", [P, 8], F32)
-            nc.scalar.activation(out=warm[:], in_=pages_a[0][:, 0:8], func=ACT.Sigmoid)
-        ident = held("ident", [P, P], F32)
         make_identity(nc, ident[:])
 
         list1 = held("list1", [P, S // 16], U16)
@@ -120,7 +126,6 @@ def tile_list_manhole_source_sink_kernel(
         w3 = held("w3", [P, H], U32)
         w5 = held("w5", [P, 2, 2 * N], U8)
         gain1 = held("gain1", [P, S], F32)
-        gain2 = held("gain2", [P, S], F32)
         w1_raw, w4_raw, level_sb = [], [], []
 
         def load_w1(c):
@@ -134,29 +139,43 @@ def tile_list_manhole_source_sink_kernel(
             load(rows[:], level[P * s : P * (s + 1), :])
             level_sb.append(rows)
 
-        load(tab[:].bitcast(I32), tab_words[0].rearrange("p t i -> p (t i)").bitcast(I32))
-        nc.sync.dma_start(list1[:], offs)
-        for q in range(4):
-            load(tab_plane[32 * q : 32 * q + 4, :].bitcast(I32), tab_scales[0, 4 * q : 4 * q + 4, :].bitcast(I32))
+        if STG:
+            staged = held("staged", [P, T // 4], I32, tag="gain2")
+            nc.sync.dma_start(list1[:], offs)
+            for q in range(4):
+                load(staged[32 * q : 32 * q + 4, :], tab_scales[0, 4 * q : 4 * q + 4, :].bitcast(I32))
+            load(tab[:].bitcast(I32), tab_words[0].rearrange("p t i -> p (t i)").bitcast(I32))
+            for q in range(4):
+                rows = slice(32 * q, 32 * q + 4)
+                nc.vector.tensor_copy(out=tab_plane[rows, :].bitcast(I32), in_=staged[rows, :])
+        else:
+            load(tab[:].bitcast(I32), tab_words[0].rearrange("p t i -> p (t i)").bitcast(I32))
+            nc.sync.dma_start(list1[:], offs)
+            for q in range(4):
+                load(tab_plane[32 * q : 32 * q + 4, :].bitcast(I32), tab_scales[0, 4 * q : 4 * q + 4, :].bitcast(I32))
+        gain2 = held("gain2", [P, S], F32)
+        if WARM:
+            warm = held("warm", [P, 8], F32)
+            nc.scalar.activation(out=warm[:], in_=pages_a[0][:, 0:8], func=ACT.Sigmoid)
         load_w1(0)
         load(w2[:].bitcast(I32), w2_words[0].bitcast(I32))
         if not PLQ:
             load_plane(nc.sync, w2_plane, w2_scales)
         nc.sync.dma_start(list2[:], offs2)
         load(gain1[:], wg1)
-        load_w4(0)
-        load(w3[:].bitcast(I32), w3_words[0].rearrange("p c i -> p (c i)").bitcast(I32))
-        if not PLQ:
-            load_plane(nc.sync, w3_plane, w3_scales)
-        load_w1(1)
-        load(gain2[:], wg2)
-        load_level(0)
-        nc.sync.dma_start(list3[:], offs3)
-        cells_raw = []
 
         def load_w5():
             load(w5[:].bitcast(I32), w5_words.rearrange("a p c -> p a c").bitcast(I32))
             load_plane(nc.sync, w5_plane, w5_scales)
+
+        load_w4(0)
+        load(w3[:].bitcast(I32), w3_words[0].rearrange("p c i -> p (c i)").bitcast(I32))
+        load_plane(nc.sync, w3_plane, w3_scales)
+        load(gain2[:], wg2)
+        nc.sync.dma_start(list3[:], offs3)
+        load_level(0)
+        load_w1(1)
+        cells_raw = []
 
         def load_cells(h):
             cells_raw.append(load_rows("cells_raw%d" % h, cells[:, HALF * h : HALF * (h + 1)]))
@@ -165,31 +184,33 @@ def tile_list_manhole_source_sink_kernel(
         jobs = {"a": load_w1, "b": load_w4, "l": load_level, "c": load_cells, "f": lambda k: load_w5(),
                 "s": lambda k: load(w6_raw[:], w6.rearrange("(p i) c -> p i c", i=PACK))}
         orders = (
-            "l1 b1 a2 l2 b2 a3 l3 b3 a4 l4 f0 s0 c0 c1 l5 l6 l7",
-            "b1 a2 b2 a3 b3 a4 l1 l2 f0 s0 l3 c0 c1 l4 l5 l6 l7",
-            "b1 a2 l1 b2 a3 b3 a4 l2 f0 s0 c0 c1 l3 l4 l5 l6 l7",
-            "b1 a2 b2 a3 b3 a4 f0 l1 s0 c0 l2 c1 l3 l4 l5 l6 l7",
-            "b1 a2 l1 b2 a3 l2 b3 a4 f0 l3 s0 l4 c0 l5 c1 l6 l7",
+            "b1 l1 a2 b2 l2 a3 b3 f0 l3 s0 l4 c0 l5 c1 l6 l7",
+            "b1 a2 l1 b2 a3 l2 b3 f0 l3 s0 l4 c0 l5 c1 l6 l7",
+            "l1 b1 a2 l2 b2 a3 l3 b3 f0 s0 l4 c0 l5 c1 l6 l7",
+            "b1 a2 b2 a3 b3 l1 l2 f0 s0 l3 c0 l4 c1 l5 l6 l7",
+            "l1 b1 f0 a2 l2 b2 a3 l3 b3 s0 l4 c0 l5 c1 l6 l7",
         )
         for job in orders[ORDER].split():
             jobs[job[0]](int(job[1]))
 
         v_codes = held("v_codes", [P, S], U32)
         v_scales = held("v_scales", [P, S], U8)
-        nc.vector.tensor_copy(v_codes[:], tab[:].indirect(list1[:]))
         nc.vector.tensor_copy(v_scales[:], tab_plane[:].indirect(list1[:]))
+        nc.vector.tensor_copy(v_codes[:], tab[:].indirect(list1[:]))
         v = (v_codes[:].bitcast(E4M3), v_scales[:])
 
         w1_q, w4_q = {}, {}
 
         def prepare(name, raw, cuts, c, table):
-            width = cuts[c + 1] - cuts[c]
-            grouped = ring.tile([P, PACK * width], BF16, name="grouped", align_bytes=64, bufs=GRP)
-            round_rows(raw[c], grouped, 0, width)
-            codes, scales = quantize("%s_%d" % (name, c), grouped, width)
-            for s in range(cuts[c] // P, cuts[c + 1] // P):
-                cols = slice(P * s - cuts[c], P * (s + 1) - cuts[c])
-                table[s] = (codes[:, cols].bitcast(E4M3), scales[:, cols])
+            whole = cuts[c + 1] - cuts[c]
+            width = P if SPLIT0 and name == "w1" and c == 0 else whole
+            for c0 in range(0, whole, width):
+                grouped = ring.tile([P, PACK * width], BF16, name="grouped", align_bytes=64, bufs=GRP)
+                round_rows(raw[c][:, :, c0 : c0 + width], grouped, 0, width)
+                codes, scales = quantize("%s_%d_%d" % (name, c, c0), grouped, width)
+                for k in range(width // P):
+                    cols = slice(P * k, P * (k + 1))
+                    table[(cuts[c] + c0) // P + k] = (codes[:, cols].bitcast(E4M3), scales[:, cols])
 
         def source_products(s):
             first, second = bank(0), bank(1)
@@ -212,7 +233,10 @@ def tile_list_manhole_source_sink_kernel(
             return third, weighted
 
         def combine(slot, pair, op):
-            h = ring.tile([P, S], F32, name=slot, bufs=SRC if slot == "sources" else SNK, align_bytes=64)
+            if slot == "last_sinks":
+                h = held(slot, [P, S], F32)
+            else:
+                h = ring.tile([P, S], F32, name=slot, bufs=SRC if slot == "sources" else SNK, align_bytes=64)
             nc.vector.tensor_tensor(out=h[:], in0=pair[0][:], in1=pair[1][:], op=op)
             return h
 
@@ -241,7 +265,7 @@ def tile_list_manhole_source_sink_kernel(
 
         def turn_back(a, h, banks, copies):
             words = z_turned[a, h][:].bitcast(F32)
-            grouped = ring.tile([P, PACK * HALF], BF16, name="z_grouped", align_bytes=64)
+            grouped = ring.tile([P, PACK * HALF], BF16, name="z_grouped", align_bytes=64, bufs=3)
             for k in range(2):
                 turned = bank(banks[k])
                 for u in range(2):
@@ -253,14 +277,17 @@ def tile_list_manhole_source_sink_kernel(
                     out=grouped[:].bitcast(F32)[:, HALF * k : HALF * (k + 1)].rearrange("p (c u) -> p c u", u=2),
                     in_=turned[:].rearrange("p (u c) -> p c u", u=2),
                 )
-            codes, scales = quantize("z%d%d" % (a, h), grouped, HALF)
+            return grouped
+
+        def moving(name, grouped, scales=None):
+            codes, scales = quantize(name, grouped, HALF, scales)
             return codes[:].bitcast(E4M3), scales[:]
 
         w5_dealt = {}
         w5_plane_dealt = held("w5_plane_dealt", [P, 2, PACK, P], U8)
 
         def deal_w5(a, tag):
-            w5_dealt[a] = ring.tile([P, PACK, 2 * P], U8, name="w5_dealt%d" % a, tag=tag, bufs=SNK, align_bytes=64)
+            w5_dealt[a] = held("w5_dealt%d" % a, [P, PACK, 2 * P], U8, tag=tag)
             nc.vector.tensor_copy(
                 out=w5_dealt[a][:].bitcast(U16),
                 in_=w5[:, a, :].bitcast(U16).rearrange("p (m t) -> p t m", t=PACK),
@@ -279,8 +306,7 @@ def tile_list_manhole_source_sink_kernel(
             grouped = held("cells_grouped%d" % h, [P, PACK * HALF], BF16)
             for k in range(2):
                 round_rows(cells_raw[h], grouped, 256 * k, 256 * (k + 1))
-            codes, scales = quantize("cells%d" % h, grouped, HALF)
-            return codes[:].bitcast(E4M3), scales[:]
+            return grouped
 
         def w5_slice(a, t):
             return w5_dealt[a][:, t, :].bitcast(E2M1), w5_plane_dealt[:, a, t, :]
@@ -325,11 +351,14 @@ def tile_list_manhole_source_sink_kernel(
             nc.scalar.activation(out=gate[:], in_=page_a[:], func=ACT.Sigmoid)
             if s > 0:
                 scatter_sinks(s - 1)
-            sinks = combine("sinks", sink_pair, ALU.mult)
+            gated = ring.tile([P, T2], F32, name="gated", bufs=GATED)
+            if LVL == 0:
+                nc.vector.tensor_tensor(out=gated[:], in0=level_sb[s][:], in1=gate[:], op=ALU.mult)
+            sinks = combine("sinks" if s + 1 < SLICES else "last_sinks", sink_pair, ALU.mult)
             if s + 1 < SLICES:
                 sink_pair = sink_products(s + 1)
-            gated = ring.tile([P, T2], F32, name="gated", bufs=GATED)
-            (nc.gpsimd if GP else nc.vector).tensor_tensor(out=gated[:], in0=level_sb[s][:], in1=gate[:], op=ALU.mult)
+            if LVL == 1:
+                nc.vector.tensor_tensor(out=gated[:], in0=level_sb[s][:], in1=gate[:], op=ALU.mult)
             if s > 0:
                 turn_into(sums, pages_b[(s - 1) % PB], False)
                 for h in range(2):
@@ -344,10 +373,12 @@ def tile_list_manhole_source_sink_kernel(
             if s == S_W6:
                 w6_codes, w6_scales = prepare_w6()
             if s == 4:
-                for h in range(2):
-                    z_q[0, h] = turn_back(0, h, (6, 7), (nc.scalar.copy, nc.scalar.copy))
-            if s in (S_CELLS, S_CELLS + 1):
-                cells_q[s - S_CELLS] = prepare_cells(s - S_CELLS)
+                z_q[0, 0] = moving("z00", turn_back(0, 0, (6, 7), (nc.scalar.copy, nc.scalar.copy)))
+                z_waiting = turn_back(0, 1, (6, 7), (nc.scalar.copy, nc.scalar.copy))
+            if s == S_CELLS:
+                cells_q[0] = moving("cells0", prepare_cells(0))
+            if s == S_CELLS + 1:
+                cells_waiting = prepare_cells(1)
 
         def open_sum(t, h, b):
             acc = bank(b)
@@ -358,39 +389,48 @@ def tile_list_manhole_source_sink_kernel(
 
         scatter_sinks(SLICES - 1)
         page_b = pages_b[(SLICES - 1) % PB]
-        deal_w5(1, "sinks")
         accs = {(t, 0): open_sum(t, 0, t) for t in range(PACK)}
         turn_into(sums, page_b, False)
         round_z(SLICES - 1, 0, sums[0], nc.scalar.copy)
-        round_z(SLICES - 1, 1, sums[1], nc.vector.tensor_copy)
-        z_q[1, 0] = turn_back(1, 0, (6, 7), (nc.scalar.copy, nc.vector.tensor_copy))
-        z_q[1, 1] = turn_back(1, 1, (4, 5), (nc.scalar.copy, nc.scalar.copy))
+        cells_q[1] = moving("cells1", cells_waiting, held("cells1_scales", [P, HALF], U8, tag="gain2"))
+        deal_w5(1, "cells_grouped1")
+        z_q[0, 1] = moving("z01", z_waiting, held("z01_scales", [P, HALF], U8, tag="last_sinks"))
+        round_z(SLICES - 1, 1, sums[1], nc.vector.tensor_copy if RZ else nc.scalar.copy)
+        z_q[1, 0] = moving("z10", turn_back(1, 0, (6, 7), (nc.scalar.copy, nc.vector.tensor_copy)))
+        z_q[1, 1] = moving("z11", turn_back(1, 1, (4, 5), (nc.scalar.copy, nc.vector.tensor_copy if WC else nc.scalar.copy)))
         for t in range(2):
             accs[t, 1] = open_sum(t, 1, 6 + t)
 
         y_rows = out_0.rearrange("(p t) c -> p t c", t=PACK)
         y_words = out_1[0].rearrange("p c t -> p (c t)").bitcast(I32)
         y_plane = held("y_plane", [P, T2], U8)
+        pieces = 0
         for h in range(2):
-            cols = slice(HALF * h, HALF * (h + 1))
-            if h == 1:
-                for t in range(2, PACK):
-                    accs[t, 1] = open_sum(t, 1, 2 + t)
-            y = held("y%d" % h, [P, PACK, HALF], F32, tag="cells_raw%d" % h)
             for t in range(PACK):
+                if h == 1 and t >= 2:
+                    accs[t, 1] = open_sum(t, 1, 2 + t)
                 mx(accs[t, h][:], w5_slice(1, t), z_q[1, h], False, True)
-                copy = nc.vector.tensor_copy if (t, h) == (1, 0) else nc.scalar.copy
-                copy(out=y[:, t, :], in_=accs[t, h][:])
-                if t % 2 == 1:
-                    nc.sync.dma_start(out=y_rows[:, t - 1 : t + 1, cols], in_=y[:, t - 1 : t + 1, :])
-            grouped = held("y_grouped%d" % h, [P, PACK * HALF], BF16, tag="cells_grouped%d" % h)
-            nc.vector.tensor_copy(
-                out=grouped[:].rearrange("p (c j t) -> p c t j", j=4, t=PACK),
-                in_=y[:].rearrange("p t (c j) -> p c t j", j=4),
-            )
-            y_codes = held("y_codes%d" % h, [P, HALF], U32)
-            nc.vector.quantize_mx(out=y_codes[:].bitcast(E4M3), scales=y_plane[:, cols], in_=grouped[:])
-            nc.sync.dma_start(out=y_words[:, cols], in_=y_codes[:].bitcast(I32))
+            cuts = Y_CUTS[h]
+            for c0, c1 in zip(cuts, cuts[1:]):
+                width = c1 - c0
+                cols = slice(HALF * h + c0, HALF * h + c1)
+                y = held("y%d" % pieces, [P, PACK, width], F32, tag="level%d" % pieces if width <= 256 else "cells_raw%d" % h)
+                for t in range(PACK):
+                    copy = nc.vector.tensor_copy if (VMASK >> (4 * pieces + t)) & 1 else nc.scalar.copy
+                    copy(out=y[:, t, :], in_=accs[t, h][:, c0:c1])
+                    if width == HALF and t % 2 == 1:
+                        nc.sync.dma_start(out=y_rows[:, t - 1 : t + 1, cols], in_=y[:, t - 1 : t + 1, :])
+                if width < HALF:
+                    nc.sync.dma_start(out=y_rows[:, :, cols], in_=y[:])
+                grouped = held("y_grouped%d" % pieces, [P, PACK * width], BF16, tag="level%d" % (4 + pieces))
+                nc.vector.tensor_copy(
+                    out=grouped[:].rearrange("p (c j t) -> p c t j", j=4, t=PACK),
+                    in_=y[:].rearrange("p t (c j) -> p c t j", j=4),
+                )
+                y_codes = held("y_codes%d" % pieces, [P, width], U32)
+                nc.vector.quantize_mx(out=y_codes[:].bitcast(E4M3), scales=y_plane[:, cols], in_=grouped[:])
+                nc.sync.dma_start(out=y_words[:, cols], in_=y_codes[:].bitcast(I32))
+                pieces = pieces + 1
         for q in range(4):
             queue = nc.sync if q % 2 == 0 else nc.scalar
             queue.dma_start(

@@ -24,19 +24,19 @@ HALF = 512
 W1_CUTS = (0, 256, 512, 768, 1024)
 W4_CUTS = (0, 256, 512, 768, 1024)
 GP = 0
-PA = 2
-PB = 1
+PA = 1
+PB = 2
 GATE = 2
 GATED = 2
 AHEAD = 4
-ORDER = 3
-S_W6 = 5
+ORDER = 2
+S_W6 = 2
 S_CELLS = 3
-S_DEAL = 5
+S_DEAL = 6
 GRP = 3
-PLQ = 1
+PLQ = 0
 WARM = 1
-PREP_POS = 0
+PREP_POS = 1
 SRC = 2
 SNK = 2
 TQ = 1
@@ -44,6 +44,19 @@ W5E = 0
 LVL = 1
 RZ = 1
 STG = 1
+PAQ = 0
+TURNED = (3, 4, 5, 6, 7)
+HB = 1
+QPOS = 0
+S_CELLS1 = 6
+SPLITL = 1
+TPOS = 1
+NSLOT = 3
+EARLY = 1
+S_TB0 = 5
+S_TB1 = 6
+CHAIN = 1
+LAST = 1
 SPLIT0 = 1
 WC = 0
 VMASK = 10
@@ -86,10 +99,12 @@ def tile_list_manhole_source_sink_kernel(
             load(raw[:], rows.rearrange("(p i) c -> p i c", i=PACK))
             return raw
 
-        def round_rows(raw, grouped, c0, c1):
-            nc.scalar.copy(
+        def round_rows(raw, grouped, c0, c1, sign=1.0):
+            nc.scalar.activation(
                 out=grouped[:, PACK * c0 : PACK * c1].rearrange("p (c j i) -> p c i j", j=4, i=PACK),
                 in_=raw[:, :, c0:c1].rearrange("p i (c j) -> p c i j", j=4),
+                func=ACT.Copy,
+                scale=sign,
             )
 
         def quantize(name, grouped, width, scales=None):
@@ -104,15 +119,24 @@ def tile_list_manhole_source_sink_kernel(
                 out=out, lhsT=lhs[0], lhsT_scale=lhs[1], rhs=rhs[0], rhs_scale=rhs[1], start=start, stop=stop
             )
 
+        if WARM:
+            warm = held("warm", [P, 16], F32)
+            nc.vector.memset(warm[:, 0:8], 0.0)
+            nc.scalar.activation(out=warm[:, 8:16], in_=warm[:, 0:8], func=ACT.Sigmoid)
         tab_plane = held("tab_plane", [P, T], U8)
-        (nc.vector if PLQ else nc.gpsimd).memset(tab_plane[:].bitcast(I32), 0)
+        nc.vector.memset(tab_plane[:].bitcast(I32), 0)
         w2_plane = zero_plane(nc.gpsimd if PLQ else nc.vector, "w2_plane", 1, H)
         w5_plane = zero_plane(nc.vector, "w5_plane", 2, N)
         w3_plane = zero_plane(nc.vector, "w3_plane", 1, H)
-        pages_a = [held("page_a%d" % k, [P, T2], F32) for k in range(PA)]
-        pages_b = [held("page_b%d" % k, [P, T2], F32) for k in range(PB)]
-        for page in pages_a + pages_b:
+        pages_a, pages_b = [], []
+
+        def zero_page(pages, name, tag):
+            page = held(name, [P, T2], F32, tag=tag)
             nc.vector.memset(page[:], 0.0)
+            pages.append(page)
+
+        if not PAQ:
+            zero_page(pages_a, "page_a", "")
         ident = held("ident", [P, P], F32)
         if PLQ:
             load_plane(nc.gpsimd, w2_plane, w2_scales)
@@ -154,27 +178,24 @@ def tile_list_manhole_source_sink_kernel(
             for q in range(4):
                 load(tab_plane[32 * q : 32 * q + 4, :].bitcast(I32), tab_scales[0, 4 * q : 4 * q + 4, :].bitcast(I32))
         gain2 = held("gain2", [P, S], F32)
-        if WARM:
-            warm = held("warm", [P, 8], F32)
-            nc.scalar.activation(out=warm[:], in_=pages_a[0][:, 0:8], func=ACT.Sigmoid)
         load_w1(0)
         load(w2[:].bitcast(I32), w2_words[0].bitcast(I32))
         if not PLQ:
             load_plane(nc.sync, w2_plane, w2_scales)
         nc.sync.dma_start(list2[:], offs2)
         load(gain1[:], wg1)
+        load_w4(0)
 
         def load_w5():
             load(w5[:].bitcast(I32), w5_words.rearrange("a p c -> p a c").bitcast(I32))
             load_plane(nc.sync, w5_plane, w5_scales)
 
-        load_w4(0)
+        load_w1(1)
         load(w3[:].bitcast(I32), w3_words[0].rearrange("p c i -> p (c i)").bitcast(I32))
         load_plane(nc.sync, w3_plane, w3_scales)
+        load_level(0)
         load(gain2[:], wg2)
         nc.sync.dma_start(list3[:], offs3)
-        load_level(0)
-        load_w1(1)
         cells_raw = []
 
         def load_cells(h):
@@ -184,11 +205,9 @@ def tile_list_manhole_source_sink_kernel(
         jobs = {"a": load_w1, "b": load_w4, "l": load_level, "c": load_cells, "f": lambda k: load_w5(),
                 "s": lambda k: load(w6_raw[:], w6.rearrange("(p i) c -> p i c", i=PACK))}
         orders = (
-            "b1 l1 a2 b2 l2 a3 b3 f0 l3 s0 l4 c0 l5 c1 l6 l7",
-            "b1 a2 l1 b2 a3 l2 b3 f0 l3 s0 l4 c0 l5 c1 l6 l7",
-            "l1 b1 a2 l2 b2 a3 l3 b3 f0 s0 l4 c0 l5 c1 l6 l7",
-            "b1 a2 b2 a3 b3 l1 l2 f0 s0 l3 c0 l4 c1 l5 l6 l7",
-            "l1 b1 f0 a2 l2 b2 a3 l3 b3 s0 l4 c0 l5 c1 l6 l7",
+            "b1 l1 a2 s0 b2 l2 a3 c0 b3 l3 c1 f0 l4 l5 l6 l7",
+            "b1 a2 l1 b2 a3 b3 s0 l2 c0 l3 c1 f0 l4 l5 l6 l7",
+            "l1 b1 a2 b2 a3 b3 s0 l2 c0 l3 c1 l4 f0 l5 l6 l7",
         )
         for job in orders[ORDER].split():
             jobs[job[0]](int(job[1]))
@@ -197,26 +216,71 @@ def tile_list_manhole_source_sink_kernel(
         v_scales = held("v_scales", [P, S], U8)
         nc.vector.tensor_copy(v_scales[:], tab_plane[:].indirect(list1[:]))
         nc.vector.tensor_copy(v_codes[:], tab[:].indirect(list1[:]))
+        if PAQ:
+            zero_page(pages_a, "page_a", "tab_plane")
         v = (v_codes[:].bitcast(E4M3), v_scales[:])
 
         w1_q, w4_q = {}, {}
 
-        def prepare(name, raw, cuts, c, table):
-            whole = cuts[c + 1] - cuts[c]
-            width = P if SPLIT0 and name == "w1" and c == 0 else whole
-            for c0 in range(0, whole, width):
-                grouped = ring.tile([P, PACK * width], BF16, name="grouped", align_bytes=64, bufs=GRP)
-                round_rows(raw[c][:, :, c0 : c0 + width], grouped, 0, width)
-                codes, scales = quantize("%s_%d_%d" % (name, c, c0), grouped, width)
-                for k in range(width // P):
-                    cols = slice(P * k, P * (k + 1))
-                    table[(cuts[c] + c0) // P + k] = (codes[:, cols].bitcast(E4M3), scales[:, cols])
+        def round_parts(name, parts, tag):
+            width = sum(raw.shape[2] for raw, table, first in parts)
+            grouped = held(name + "_grouped", [P, PACK * width], BF16, tag=tag)
+            at = 0
+            for raw, table, first in parts:
+                sign = -1.0 if table is w1_q and first in TURNED else 1.0
+                round_rows(raw, grouped[:, PACK * at : PACK * (at + raw.shape[2])], 0, raw.shape[2], sign)
+                at = at + raw.shape[2]
+
+            def finish():
+                codes, scales = quantize(name, grouped, width)
+                at = 0
+                for raw, table, first in parts:
+                    for k in range(raw.shape[2] // P):
+                        cols = slice(at + P * k, at + P * (k + 1))
+                        table[first + k] = (codes[:, cols].bitcast(E4M3), scales[:, cols])
+                    at = at + raw.shape[2]
+
+            return finish
+
+        def round_pair(k):
+            parts = [(w4_raw[k][:], w4_q, 2 * k)]
+            if k + 1 < len(w1_raw):
+                s = 2 * k + 2
+                if (s in TURNED) == (s + 1 in TURNED):
+                    parts.append((w1_raw[k + 1][:], w1_q, s))
+                else:
+                    parts.append((w1_raw[k + 1][:, :, 0:P], w1_q, s))
+                    parts.append((w1_raw[k + 1][:, :, P : 2 * P], w1_q, s + 1))
+            return round_parts("pair%d" % k, parts, "second_first")
 
         def source_products(s):
             first, second = bank(0), bank(1)
+            if s in TURNED:
+                w2_s = (w2[:, 2 * P * s : 2 * P * (s + 1)].bitcast(E2M1), w2_plane[:, 0, P * s : P * (s + 1)])
+                blocks = [slice(P * b, P * (b + 1)) for b in range(S // P)]
+                for cols in blocks:
+                    v_b = (v_codes[:, cols].bitcast(E4M3), v_scales[:, cols])
+                    mx(second[:, cols], v_b, w2_s, True, False)
+                    mx(second[:, cols], v_b, w1_q[s], False, True)
+                    mx(first[:, cols], v_b, w1_q[s])
+                excess = ring.tile([P, S], F32, name="excess", bufs=1)
+                nc.scalar.activation(out=excess[:], in_=second[:], func=ACT.Relu)
+                base = ring.tile([P, S], F32, name="base", bufs=1)
+                nc.scalar.activation(out=base[:], in_=first[:], func=ACT.Copy, scale=-1.0)
+                larger = bank(HB)
+                for cols in blocks:
+                    for rows, start in ((excess, True), (base, False)):
+                        nc.tensor.matmul(
+                            larger[:, cols], lhsT=rows[:, cols], rhs=ident[:], is_transpose=True, start=start, stop=not start
+                        )
+                if EARLY:
+                    h = held("features%d" % (s % NSLOT), [P, S], F32)
+                    nc.scalar.copy(out=h[:], in_=larger[:])
+                    return None, h
+                return larger, None
             mx(second[:], (w2[:, 2 * P * s : 2 * P * (s + 1)].bitcast(E2M1), w2_plane[:, 0, P * s : P * (s + 1)]), v)
             mx(first[:], w1_q[s], v)
-            second_sb = ring.tile([P, S], F32, name="second_sb")
+            second_sb = held("second_first", [P, S], F32) if s == 0 else ring.tile([P, S], F32, name="second_sb")
             nc.scalar.copy(out=second_sb[:], in_=second[:])
             return first, second_sb
 
@@ -233,15 +297,17 @@ def tile_list_manhole_source_sink_kernel(
             return third, weighted
 
         def combine(slot, pair, op):
-            if slot == "last_sinks":
-                h = held(slot, [P, S], F32)
+            if pair[0] is None:
+                return pair[1]
+            h = held(slot, [P, S], F32)
+            if pair[1] is None:
+                nc.scalar.copy(out=h[:], in_=pair[0][:])
             else:
-                h = ring.tile([P, S], F32, name=slot, bufs=SRC if slot == "sources" else SNK, align_bytes=64)
-            nc.vector.tensor_tensor(out=h[:], in0=pair[0][:], in1=pair[1][:], op=op)
+                nc.vector.tensor_tensor(out=h[:], in0=pair[0][:], in1=pair[1][:], op=op)
             return h
 
-        def turn_into(sums, rows, first):
-            for b in range(T2 // P):
+        def turn_into(sums, rows, first, blocks=range(T2 // P)):
+            for b in blocks:
                 nc.tensor.matmul(
                     sums[b // 4][:, P * (b % 4) : P * (b % 4 + 1)],
                     lhsT=rows[:, P * b : P * (b + 1)],
@@ -255,7 +321,7 @@ def tile_list_manhole_source_sink_kernel(
 
         def round_z(s, h, sums, copy):
             if s % 4 == 0:
-                z_turned[s // 4, h] = held("z_turned%d" % h, [P, 4 * HALF], BF16)
+                z_turned[s // 4, h] = held("z_turned%d%d" % (s // 4, h), [P, 4 * HALF], BF16)
             copy(
                 out=z_turned[s // 4, h][:].rearrange("t (u b s q e) -> t u b s q e", u=2, b=4, s=4, e=2)[
                     :, :, :, s % 4, :, :
@@ -284,7 +350,6 @@ def tile_list_manhole_source_sink_kernel(
             return codes[:].bitcast(E4M3), scales[:]
 
         w5_dealt = {}
-        w5_plane_dealt = held("w5_plane_dealt", [P, 2, PACK, P], U8)
 
         def deal_w5(a, tag):
             w5_dealt[a] = held("w5_dealt%d" % a, [P, PACK, 2 * P], U8, tag=tag)
@@ -294,16 +359,16 @@ def tile_list_manhole_source_sink_kernel(
             )
 
         def prepare_w6():
-            grouped = held("w6_grouped", [P, PACK * N], BF16)
+            grouped = held("w6_grouped", [P, PACK * N], BF16, tag="level0")
             for k in range(2):
                 nc.scalar.copy(
                     out=grouped[:].rearrange("p (t m i) -> p m i t", t=PACK, i=PACK)[:, 64 * k : 64 * (k + 1)],
                     in_=w6_raw[:].rearrange("p i (m t) -> p m i t", t=PACK)[:, 64 * k : 64 * (k + 1)],
                 )
-            return quantize("w6", grouped, N)
+            return grouped
 
         def prepare_cells(h):
-            grouped = held("cells_grouped%d" % h, [P, PACK * HALF], BF16)
+            grouped = held("cells_grouped%d" % h, [P, PACK * HALF], BF16, tag="level%d" % (1 + h))
             for k in range(2):
                 round_rows(cells_raw[h], grouped, 256 * k, 256 * (k + 1))
             return grouped
@@ -313,72 +378,90 @@ def tile_list_manhole_source_sink_kernel(
 
         z_q, cells_q = {}, {}
 
-        def prepare_ahead(s):
-            if P * s in W1_CUTS[:-1]:
-                prepare("w1", w1_raw, W1_CUTS, W1_CUTS.index(P * s), w1_q)
-            if P * (s - 1) in W4_CUTS[:-1]:
-                prepare("w4", w4_raw, W4_CUTS, W4_CUTS.index(P * (s - 1)), w4_q)
-
-        prepare_ahead(0)
-        sources = combine("sources", source_products(0), ALU.max)
-        prepare_ahead(1)
-        source_pair = source_products(1)
-        sink_pair = sink_products(0)
-        sums = None
-
-        def prep(s):
-            for k in range(2 if s == 0 else s + AHEAD, s + AHEAD + 1):
-                prepare_ahead(k)
-
         def scatter_sinks(s):
-            if GP:
-                nc.vector.tensor_copy(pages_b[s % PB][:].indirect(list3[:]), sinks[:])
-            else:
-                nc.vector.tensor_tensor(pages_b[s % PB][:].indirect(list3[:]), sinks[:], gain2[:], ALU.mult)
+            nc.vector.tensor_tensor(pages_b[s % PB][:].indirect(list3[:]), sinks[:], gain2[:], ALU.mult)
 
-        for s in range(SLICES):
-            page_a = pages_a[s % PA]
-            if PREP_POS == 0:
-                prep(s)
-            nc.vector.tensor_tensor(page_a[:].indirect(list2[:]), sources[:], gain1[:], ALU.mult)
+        page_a = pages_a[0]
+        for s in range(2):
+            round_parts("w1_slice%d" % s, [(w1_raw[0][:, :, P * s : P * (s + 1)], w1_q, s)], "")()
+        sources = {0: combine("features0", source_products(0), ALU.max)}
+        zero_page(pages_b, "page_b0", "tab")
+        if PB == 2:
+            zero_page(pages_b, "page_b1", "w1_raw0")
+        source_pairs = {1: source_products(1)}
+        pending = [round_pair(0)]
+        later = {}
+        gates = {}
+
+        def gate_level(s, halves, gated, sums):
+            for h in halves:
+                cols = slice(HALF * h, HALF * (h + 1))
+                nc.vector.tensor_tensor(out=gated[:, cols], in0=level_sb[s][:, cols], in1=gates[s][:, cols], op=ALU.mult)
+                turn_into(sums, gated, True, range(4 * h, 4 * h + 4))
+
+        def finish_pending():
+            for finish in pending:
+                finish()
+            pending.clear()
+
+        for s in range(SLICES + 1):
+            if s < SLICES:
+                nc.vector.tensor_tensor(page_a[:].indirect(list2[:]), sources[s][:], gain1[:], ALU.mult)
+                gates[s] = ring.tile([P, T2], F32, name="gate", bufs=GATE)
+                nc.scalar.activation(out=gates[s][:], in_=page_a[:], func=ACT.Sigmoid)
             if s + 1 < SLICES:
-                sources = combine("sources", source_pair, ALU.max)
-            if PREP_POS == 1:
-                prep(s)
-            if s + 2 < SLICES:
-                source_pair = source_products(s + 2)
-            gate = ring.tile([P, T2], F32, name="gate", bufs=GATE)
-            nc.scalar.activation(out=gate[:], in_=page_a[:], func=ACT.Sigmoid)
+                sources[s + 1] = combine("features%d" % ((s + 1) % NSLOT), source_pairs[s + 1], ALU.max)
+            if QPOS == 0 or s == 0:
+                finish_pending()
+            if s + 2 < SLICES and TPOS == 0:
+                source_pairs[s + 2] = source_products(s + 2)
+            if s > 0:
+                gated = ring.tile([P, T2], F32, name="gated", bufs=GATED)
+                sums = [bank(4), bank(5)]
+                if s == SLICES:
+                    sinks = combine("last_sinks", sink_pair, ALU.mult)
+                    gate_level(s - 1, (0, 1), gated, sums)
+                else:
+                    gate_level(s - 1, (0,), gated, sums)
+                    sinks = combine("features%d" % (s % NSLOT), sink_pair, ALU.mult)
+            if s < SLICES:
+                sink_pair = sink_products(s)
+            if s + 2 < SLICES and TPOS == 1:
+                source_pairs[s + 2] = source_products(s + 2)
+            if 0 < s < SLICES:
+                gate_level(s - 1, (1,), gated, sums)
+            if QPOS == 1:
+                finish_pending()
+            if s == SLICES:
+                break
+            if s in (1, 3, 5):
+                pending.append(round_pair(s // 2 + 1))
+            if s == S_W6:
+                w6_grouped = prepare_w6()
+                pending.append(lambda: later.setdefault("w6", quantize("w6", w6_grouped, N)))
+            if s == S_CELLS:
+                cells_grouped = prepare_cells(0)
+                pending.append(lambda: cells_q.setdefault(0, moving("cells0", cells_grouped)))
+            if s == S_CELLS1:
+                cells_waiting = prepare_cells(1)
+            if s == S_TB0:
+                z_grouped = turn_back(0, 0, (6, 7), (nc.scalar.copy, nc.scalar.copy))
+                pending.append(lambda: z_q.setdefault((0, 0), moving("z00", z_grouped)))
+            if s == S_TB1:
+                z_waiting = turn_back(0, 1, (6, 7), (nc.scalar.copy, nc.scalar.copy))
             if s > 0:
                 scatter_sinks(s - 1)
-            gated = ring.tile([P, T2], F32, name="gated", bufs=GATED)
-            if LVL == 0:
-                nc.vector.tensor_tensor(out=gated[:], in0=level_sb[s][:], in1=gate[:], op=ALU.mult)
-            sinks = combine("sinks" if s + 1 < SLICES else "last_sinks", sink_pair, ALU.mult)
-            if s + 1 < SLICES:
-                sink_pair = sink_products(s + 1)
-            if LVL == 1:
-                nc.vector.tensor_tensor(out=gated[:], in0=level_sb[s][:], in1=gate[:], op=ALU.mult)
-            if s > 0:
                 turn_into(sums, pages_b[(s - 1) % PB], False)
                 for h in range(2):
                     round_z(s - 1, h, sums[h], nc.scalar.copy)
-            sums = [bank(4), bank(5)]
-            turn_into(sums, gated, True)
             if s == S_DEAL:
-                deal_w5(0, "w5_dealt0")
+                deal_w5(0, "level3")
+                w5_plane_dealt = held("w5_plane_dealt", [P, 2, PACK, P], U8, tag="level4")
                 nc.vector.tensor_copy(
                     out=w5_plane_dealt[:], in_=w5_plane[:].rearrange("p a (m t) -> p a t m", t=PACK)
                 )
-            if s == S_W6:
-                w6_codes, w6_scales = prepare_w6()
-            if s == 4:
-                z_q[0, 0] = moving("z00", turn_back(0, 0, (6, 7), (nc.scalar.copy, nc.scalar.copy)))
-                z_waiting = turn_back(0, 1, (6, 7), (nc.scalar.copy, nc.scalar.copy))
-            if s == S_CELLS:
-                cells_q[0] = moving("cells0", prepare_cells(0))
-            if s == S_CELLS + 1:
-                cells_waiting = prepare_cells(1)
+        finish_pending()
+        w6_codes, w6_scales = later["w6"]
 
         def open_sum(t, h, b):
             acc = bank(b)
@@ -393,7 +476,7 @@ def tile_list_manhole_source_sink_kernel(
         turn_into(sums, page_b, False)
         round_z(SLICES - 1, 0, sums[0], nc.scalar.copy)
         cells_q[1] = moving("cells1", cells_waiting, held("cells1_scales", [P, HALF], U8, tag="gain2"))
-        deal_w5(1, "cells_grouped1")
+        deal_w5(1, "level2")
         z_q[0, 1] = moving("z01", z_waiting, held("z01_scales", [P, HALF], U8, tag="last_sinks"))
         round_z(SLICES - 1, 1, sums[1], nc.vector.tensor_copy if RZ else nc.scalar.copy)
         z_q[1, 0] = moving("z10", turn_back(1, 0, (6, 7), (nc.scalar.copy, nc.vector.tensor_copy)))
@@ -414,7 +497,7 @@ def tile_list_manhole_source_sink_kernel(
             for c0, c1 in zip(cuts, cuts[1:]):
                 width = c1 - c0
                 cols = slice(HALF * h + c0, HALF * h + c1)
-                y = held("y%d" % pieces, [P, PACK, width], F32, tag="level%d" % pieces if width <= 256 else "cells_raw%d" % h)
+                y = held("y%d" % pieces, [P, PACK, width], F32, tag="w4_raw%d" % pieces if width <= 256 else "cells_raw%d" % h)
                 for t in range(PACK):
                     copy = nc.vector.tensor_copy if (VMASK >> (4 * pieces + t)) & 1 else nc.scalar.copy
                     copy(out=y[:, t, :], in_=accs[t, h][:, c0:c1])
@@ -422,7 +505,7 @@ def tile_list_manhole_source_sink_kernel(
                         nc.sync.dma_start(out=y_rows[:, t - 1 : t + 1, cols], in_=y[:, t - 1 : t + 1, :])
                 if width < HALF:
                     nc.sync.dma_start(out=y_rows[:, :, cols], in_=y[:])
-                grouped = held("y_grouped%d" % pieces, [P, PACK * width], BF16, tag="level%d" % (4 + pieces))
+                grouped = held("y_grouped%d" % pieces, [P, PACK * width], BF16, tag=("level6", "level7", "w1_raw1", "w1_raw2")[pieces])
                 nc.vector.tensor_copy(
                     out=grouped[:].rearrange("p (c j t) -> p c t j", j=4, t=PACK),
                     in_=y[:].rearrange("p t (c j) -> p c t j", j=4),

@@ -19,48 +19,20 @@ ACT = mybir.ActivationFunctionType
 
 P = 128
 PACK = 4
+QUADRANTS = 4
+LINE = 4
 SLICES = H // P
+SLICES_A_PASS = 4
 HALF = 512
-W1_CUTS = (0, 256, 512, 768, 1024)
-W4_CUTS = (0, 256, 512, 768, 1024)
-GP = 0
-PA = 1
-PB = 2
-GATE = 2
-GATED = 2
-AHEAD = 4
-ORDER = 2
-S_W6 = 2
-S_CELLS = 3
-S_DEAL = 6
-GRP = 3
-PLQ = 0
-WARM = 1
-PREP_POS = 1
-SRC = 2
-SNK = 2
-TQ = 1
-W5E = 0
-LVL = 1
-RZ = 1
-STG = 1
-PAQ = 0
-TURNED = (3, 4, 5, 6, 7)
-HB = 1
-QPOS = 0
-S_CELLS1 = 6
-SPLITL = 1
-TPOS = 1
-NSLOT = 3
-EARLY = 1
-S_TB0 = 5
-S_TB1 = 6
-CHAIN = 1
-LAST = 1
-SPLIT0 = 1
-WC = 0
-VMASK = 10
-Y_CUTS = ((0, 512), (0, 512))
+BLOCKS = HALF // P
+CHUNK = 2 * P
+
+RELU_SLICES = range(2, 7)
+FEATURE_TILES = 3
+CELLS_STEP = 3
+TURN_STEP = SLICES_A_PASS + 1
+DEAL_STEP = 6
+SCALAR_SHARE = 192
 
 
 def tile_list_manhole_source_sink_kernel(
@@ -73,8 +45,8 @@ def tile_list_manhole_source_sink_kernel(
         ring = ctx.enter_context(tc.tile_pool(name="ring", bufs=2))
         psum = ctx.enter_context(tc.psum_pool(name="psum", bufs=1))
 
-        def held(name, shape, dtype, tag=""):
-            return keep.tile(shape, dtype, name=name, tag=tag or name, align_bytes=64)
+        def held(name, shape, dtype, after=""):
+            return keep.tile(shape, dtype, name=name, tag=after or name, align_bytes=64)
 
         def bank(b):
             return psum.tile([P, HALF], F32, name="bank%d" % b)
@@ -82,64 +54,71 @@ def tile_list_manhole_source_sink_kernel(
         def load(tile_ap, dram_ap):
             nc.sync.dma_start(out=tile_ap, in_=dram_ap)
 
-        def load_plane(queue, plane, scales):
-            for q in range(4):
-                queue.dma_start(
-                    out=plane[32 * q : 32 * q + 4].bitcast(I32),
-                    in_=scales[:, 4 * q : 4 * q + 4, :].rearrange("a r c -> r a c").bitcast(I32),
-                )
+        def live_rows(q):
+            return slice(32 * q, 32 * q + 4)
 
-        def zero_plane(engine, name, passes, width):
+        def zero_plane(name, passes, width):
             plane = held(name, [P, passes, width], U8)
-            engine.memset(plane[:].rearrange("p a c -> p (a c)").bitcast(I32), 0)
+            nc.vector.memset(plane[:].rearrange("p a c -> p (a c)").bitcast(I32), 0)
             return plane
+
+        def load_plane(plane, scales):
+            for q in range(QUADRANTS):
+                rows = scales[:, 4 * q : 4 * q + 4, :].rearrange("a r c -> r a c")
+                load(plane[live_rows(q)].bitcast(I32), rows.bitcast(I32))
 
         def load_rows(name, rows):
             raw = held(name, [P, PACK, rows.shape[1]], F32)
             load(raw[:], rows.rearrange("(p i) c -> p i c", i=PACK))
             return raw
 
-        def round_rows(raw, grouped, c0, c1, sign=1.0):
-            nc.scalar.activation(
-                out=grouped[:, PACK * c0 : PACK * c1].rearrange("p (c j i) -> p c i j", j=4, i=PACK),
-                in_=raw[:, :, c0:c1].rearrange("p i (c j) -> p c i j", j=4),
-                func=ACT.Copy,
-                scale=sign,
+        def interleaved(grouped, raw):
+            return (
+                grouped.rearrange("p (c j i) -> p c i j", j=LINE, i=PACK),
+                raw.rearrange("p i (c j) -> p c i j", j=LINE),
             )
 
-        def quantize(name, grouped, width, scales=None):
+        def round_rows(grouped, raw, sign=1.0):
+            out, in_ = interleaved(grouped, raw)
+            nc.scalar.activation(out=out, in_=in_, func=ACT.Copy, scale=sign)
+
+        def quantize(name, grouped, width, scales_after=""):
+            scales = held(name + "_scales", [P, width], U8, after=scales_after)
             codes = held(name + "_codes", [P, width], U32)
-            if scales is None:
-                scales = held(name + "_scales", [P, width], U8)
             nc.vector.quantize_mx(out=codes[:].bitcast(E4M3), scales=scales[:], in_=grouped[:])
             return codes, scales
+
+        def columns(operand, cols=slice(None)):
+            codes, scales = operand
+            return codes[:, cols].bitcast(E4M3), scales[:, cols]
 
         def mx(out, lhs, rhs, start=True, stop=True):
             nc.tensor.matmul_mx(
                 out=out, lhsT=lhs[0], lhsT_scale=lhs[1], rhs=rhs[0], rhs_scale=rhs[1], start=start, stop=stop
             )
 
-        if WARM:
-            warm = held("warm", [P, 16], F32)
-            nc.vector.memset(warm[:, 0:8], 0.0)
-            nc.scalar.activation(out=warm[:, 8:16], in_=warm[:, 0:8], func=ACT.Sigmoid)
+        def block(b):
+            return slice(P * b, P * (b + 1))
+
+        def add_turned(out, rows, start, stop):
+            nc.tensor.matmul(out, lhsT=rows, rhs=ident[:], is_transpose=True, start=start, stop=stop)
+
+        def zero_page(engine, name, after=""):
+            page = held(name, [P, T2], F32, after=after)
+            engine.memset(page[:], 0.0)
+            return page
+
+        warm = held("warm", [P, 16], F32)
+        nc.vector.memset(warm[:, 0:8], 0.0)
+        nc.scalar.activation(out=warm[:, 8:16], in_=warm[:, 0:8], func=ACT.Sigmoid)
+
         tab_plane = held("tab_plane", [P, T], U8)
         nc.vector.memset(tab_plane[:].bitcast(I32), 0)
-        w2_plane = zero_plane(nc.gpsimd if PLQ else nc.vector, "w2_plane", 1, H)
-        w5_plane = zero_plane(nc.vector, "w5_plane", 2, N)
-        w3_plane = zero_plane(nc.vector, "w3_plane", 1, H)
-        pages_a, pages_b = [], []
-
-        def zero_page(pages, name, tag):
-            page = held(name, [P, T2], F32, tag=tag)
-            nc.vector.memset(page[:], 0.0)
-            pages.append(page)
-
-        if not PAQ:
-            zero_page(pages_a, "page_a", "")
+        w2_plane = zero_plane("w2_plane", 1, H)
+        w5_plane = zero_plane("w5_plane", 2, N)
+        w3_plane = zero_plane("w3_plane", 1, H)
+        first_source_page = zero_page(nc.vector, "first_source_page")
         ident = held("ident", [P, P], F32)
-        if PLQ:
-            load_plane(nc.gpsimd, w2_plane, w2_scales)
         make_identity(nc, ident[:])
 
         list1 = held("list1", [P, S // 16], U16)
@@ -150,183 +129,158 @@ def tile_list_manhole_source_sink_kernel(
         w3 = held("w3", [P, H], U32)
         w5 = held("w5", [P, 2, 2 * N], U8)
         gain1 = held("gain1", [P, S], F32)
-        w1_raw, w4_raw, level_sb = [], [], []
+        w1_raw, w4_raw, level_rows, cells_raw = [], [], [], []
 
         def load_w1(c):
-            w1_raw.append(load_rows("w1_raw%d" % c, w1[:, W1_CUTS[c] : W1_CUTS[c + 1]]))
+            w1_raw.append(load_rows("w1_raw%d" % c, w1[:, CHUNK * c : CHUNK * (c + 1)]))
 
         def load_w4(c):
-            w4_raw.append(load_rows("w4_raw%d" % c, w4[:, W4_CUTS[c] : W4_CUTS[c + 1]]))
+            w4_raw.append(load_rows("w4_raw%d" % c, w4[:, CHUNK * c : CHUNK * (c + 1)]))
 
         def load_level(s):
             rows = held("level%d" % s, [P, T2], F32)
-            load(rows[:], level[P * s : P * (s + 1), :])
-            level_sb.append(rows)
+            load(rows[:], level[block(s), :])
+            level_rows.append(rows)
 
-        if STG:
-            staged = held("staged", [P, T // 4], I32, tag="gain2")
-            nc.sync.dma_start(list1[:], offs)
-            for q in range(4):
-                load(staged[32 * q : 32 * q + 4, :], tab_scales[0, 4 * q : 4 * q + 4, :].bitcast(I32))
-            load(tab[:].bitcast(I32), tab_words[0].rearrange("p t i -> p (t i)").bitcast(I32))
-            for q in range(4):
-                rows = slice(32 * q, 32 * q + 4)
-                nc.vector.tensor_copy(out=tab_plane[rows, :].bitcast(I32), in_=staged[rows, :])
-        else:
-            load(tab[:].bitcast(I32), tab_words[0].rearrange("p t i -> p (t i)").bitcast(I32))
-            nc.sync.dma_start(list1[:], offs)
-            for q in range(4):
-                load(tab_plane[32 * q : 32 * q + 4, :].bitcast(I32), tab_scales[0, 4 * q : 4 * q + 4, :].bitcast(I32))
+        staged = held("staged", [P, T // 4], I32, after="gain2")
+        nc.sync.dma_start(list1[:], offs)
+        for q in range(QUADRANTS):
+            load(staged[live_rows(q), :], tab_scales[0, 4 * q : 4 * q + 4, :].bitcast(I32))
+        load(tab[:].bitcast(I32), tab_words[0].rearrange("p t i -> p (t i)").bitcast(I32))
+        for q in range(QUADRANTS):
+            nc.vector.tensor_copy(out=tab_plane[live_rows(q), :].bitcast(I32), in_=staged[live_rows(q), :])
         gain2 = held("gain2", [P, S], F32)
         load_w1(0)
         load(w2[:].bitcast(I32), w2_words[0].bitcast(I32))
-        if not PLQ:
-            load_plane(nc.sync, w2_plane, w2_scales)
+        load_plane(w2_plane, w2_scales)
+        load_w4(0)
         nc.sync.dma_start(list2[:], offs2)
         load(gain1[:], wg1)
-        load_w4(0)
-
-        def load_w5():
-            load(w5[:].bitcast(I32), w5_words.rearrange("a p c -> p a c").bitcast(I32))
-            load_plane(nc.sync, w5_plane, w5_scales)
-
         load_w1(1)
         load(w3[:].bitcast(I32), w3_words[0].rearrange("p c i -> p (c i)").bitcast(I32))
-        load_plane(nc.sync, w3_plane, w3_scales)
+        load_plane(w3_plane, w3_scales)
         load_level(0)
-        load(gain2[:], wg2)
         nc.sync.dma_start(list3[:], offs3)
-        cells_raw = []
-
-        def load_cells(h):
+        load(gain2[:], wg2)
+        load_level(1)
+        for c in range(1, H // CHUNK):
+            load_w4(c)
+            if c + 1 < H // CHUNK:
+                load_w1(c + 1)
+        for h in range(2):
+            load_level(2 + h)
             cells_raw.append(load_rows("cells_raw%d" % h, cells[:, HALF * h : HALF * (h + 1)]))
-
-        w6_raw = held("w6_raw", [P, PACK, N], F32)
-        jobs = {"a": load_w1, "b": load_w4, "l": load_level, "c": load_cells, "f": lambda k: load_w5(),
-                "s": lambda k: load(w6_raw[:], w6.rearrange("(p i) c -> p i c", i=PACK))}
-        orders = (
-            "b1 l1 a2 s0 b2 l2 a3 c0 b3 l3 c1 f0 l4 l5 l6 l7",
-            "b1 a2 l1 b2 a3 b3 s0 l2 c0 l3 c1 f0 l4 l5 l6 l7",
-            "l1 b1 a2 b2 a3 b3 s0 l2 c0 l3 c1 l4 f0 l5 l6 l7",
-        )
-        for job in orders[ORDER].split():
-            jobs[job[0]](int(job[1]))
+        load_level(4)
+        w6_raw = load_rows("w6_raw", w6)
+        load_level(5)
+        load(w5[:].bitcast(I32), w5_words.rearrange("a p c -> p a c").bitcast(I32))
+        load_plane(w5_plane, w5_scales)
+        load_level(6)
+        load_level(7)
 
         v_codes = held("v_codes", [P, S], U32)
         v_scales = held("v_scales", [P, S], U8)
         nc.vector.tensor_copy(v_scales[:], tab_plane[:].indirect(list1[:]))
         nc.vector.tensor_copy(v_codes[:], tab[:].indirect(list1[:]))
-        if PAQ:
-            zero_page(pages_a, "page_a", "tab_plane")
-        v = (v_codes[:].bitcast(E4M3), v_scales[:])
+        v = (v_codes, v_scales)
 
         w1_q, w4_q = {}, {}
 
-        def round_parts(name, parts, tag):
-            width = sum(raw.shape[2] for raw, table, first in parts)
-            grouped = held(name + "_grouped", [P, PACK * width], BF16, tag=tag)
-            at = 0
-            for raw, table, first in parts:
-                sign = -1.0 if table is w1_q and first in TURNED else 1.0
-                round_rows(raw, grouped[:, PACK * at : PACK * (at + raw.shape[2])], 0, raw.shape[2], sign)
-                at = at + raw.shape[2]
+        def round_weights(name, parts, after=""):
+            width = sum(raw.shape[2] for raw, table, first, sign in parts)
+            grouped = held(name + "_grouped", [P, PACK * width], BF16, after=after)
+            starts = [0]
+            for raw, table, first, sign in parts:
+                starts.append(starts[-1] + raw.shape[2])
+                round_rows(grouped[:, PACK * starts[-2] : PACK * starts[-1]], raw, sign)
 
             def finish():
-                codes, scales = quantize(name, grouped, width)
-                at = 0
-                for raw, table, first in parts:
+                operand = quantize(name, grouped, width)
+                for start, (raw, table, first, sign) in zip(starts, parts):
                     for k in range(raw.shape[2] // P):
-                        cols = slice(at + P * k, at + P * (k + 1))
-                        table[first + k] = (codes[:, cols].bitcast(E4M3), scales[:, cols])
-                    at = at + raw.shape[2]
+                        table[first + k] = columns(operand, slice(start + P * k, start + P * (k + 1)))
 
             return finish
 
-        def round_pair(k):
-            parts = [(w4_raw[k][:], w4_q, 2 * k)]
-            if k + 1 < len(w1_raw):
-                s = 2 * k + 2
-                if (s in TURNED) == (s + 1 in TURNED):
-                    parts.append((w1_raw[k + 1][:], w1_q, s))
+        def w1_sign(s):
+            return -1.0 if s in RELU_SLICES else 1.0
+
+        def round_pair(c):
+            parts = [(w4_raw[c][:], w4_q, 2 * c, 1.0)]
+            if c + 1 < len(w1_raw):
+                s = 2 * c + 2
+                if w1_sign(s) == w1_sign(s + 1):
+                    parts.append((w1_raw[c + 1][:], w1_q, s, w1_sign(s)))
                 else:
-                    parts.append((w1_raw[k + 1][:, :, 0:P], w1_q, s))
-                    parts.append((w1_raw[k + 1][:, :, P : 2 * P], w1_q, s + 1))
-            return round_parts("pair%d" % k, parts, "second_first")
+                    parts.extend((w1_raw[c + 1][:, :, block(k)], w1_q, s + k, w1_sign(s + k)) for k in range(2))
+            return round_weights("pair%d" % c, parts, after="first_b")
+
+        def features(turn):
+            return held("features%d" % (turn % FEATURE_TILES), [P, S], F32)
+
+        def w2_slice(s):
+            return w2[:, 2 * P * s : 2 * P * (s + 1)].bitcast(E2M1), w2_plane[:, 0, block(s)]
 
         def source_products(s):
-            first, second = bank(0), bank(1)
-            if s in TURNED:
-                w2_s = (w2[:, 2 * P * s : 2 * P * (s + 1)].bitcast(E2M1), w2_plane[:, 0, P * s : P * (s + 1)])
-                blocks = [slice(P * b, P * (b + 1)) for b in range(S // P)]
-                for cols in blocks:
-                    v_b = (v_codes[:, cols].bitcast(E4M3), v_scales[:, cols])
-                    mx(second[:, cols], v_b, w2_s, True, False)
-                    mx(second[:, cols], v_b, w1_q[s], False, True)
-                    mx(first[:, cols], v_b, w1_q[s])
-                excess = ring.tile([P, S], F32, name="excess", bufs=1)
-                nc.scalar.activation(out=excess[:], in_=second[:], func=ACT.Relu)
-                base = ring.tile([P, S], F32, name="base", bufs=1)
-                nc.scalar.activation(out=base[:], in_=first[:], func=ACT.Copy, scale=-1.0)
-                larger = bank(HB)
-                for cols in blocks:
-                    for rows, start in ((excess, True), (base, False)):
-                        nc.tensor.matmul(
-                            larger[:, cols], lhsT=rows[:, cols], rhs=ident[:], is_transpose=True, start=start, stop=not start
-                        )
-                if EARLY:
-                    h = held("features%d" % (s % NSLOT), [P, S], F32)
-                    nc.scalar.copy(out=h[:], in_=larger[:])
-                    return None, h
-                return larger, None
-            mx(second[:], (w2[:, 2 * P * s : 2 * P * (s + 1)].bitcast(E2M1), w2_plane[:, 0, P * s : P * (s + 1)]), v)
-            mx(first[:], w1_q[s], v)
-            second_sb = held("second_first", [P, S], F32) if s == 0 else ring.tile([P, S], F32, name="second_sb")
-            nc.scalar.copy(out=second_sb[:], in_=second[:])
-            return first, second_sb
+            a, b = bank(0), bank(1)
+            mx(b[:], w2_slice(s), columns(v))
+            mx(a[:], w1_q[s], columns(v))
+            b_rows = held("first_b", [P, S], F32) if s == 0 else ring.tile([P, S], F32, name="b_rows")
+            nc.scalar.copy(out=b_rows[:], in_=b[:])
+            return a, b_rows
+
+        def sources_by_relu(s):
+            minus_a, excess = bank(0), bank(1)
+            for b in range(BLOCKS):
+                v_block = columns(v, block(b))
+                mx(excess[:, block(b)], v_block, w2_slice(s), True, False)
+                mx(excess[:, block(b)], v_block, w1_q[s], False, True)
+                mx(minus_a[:, block(b)], v_block, w1_q[s])
+            excess_rows = ring.tile([P, S], F32, name="excess_rows", bufs=1)
+            nc.scalar.activation(out=excess_rows[:], in_=excess[:], func=ACT.Relu)
+            a_rows = ring.tile([P, S], F32, name="a_rows", bufs=1)
+            nc.scalar.activation(out=a_rows[:], in_=minus_a[:], func=ACT.Copy, scale=-1.0)
+            larger = bank(6)
+            for b in range(BLOCKS):
+                add_turned(larger[:, block(b)], excess_rows[:, block(b)], True, False)
+                add_turned(larger[:, block(b)], a_rows[:, block(b)], False, True)
+            h1 = features(s)
+            nc.scalar.copy(out=h1[:], in_=larger[:])
+            return h1
 
         def sink_products(s):
-            third, fourth = bank(2), bank(3)
-            mx(fourth[:], w4_q[s], v)
-            mx(third[:], (w3[:, P * s : P * (s + 1)].bitcast(E4M3), w3_plane[:, 0, P * s : P * (s + 1)]), v)
+            plain, inner = bank(2), bank(3)
+            mx(inner[:], w4_q[s], columns(v))
+            mx(plain[:], (w3[:, block(s)].bitcast(E4M3), w3_plane[:, 0, block(s)]), columns(v))
             squashed = ring.tile([P, S], F32, name="squashed")
-            nc.scalar.activation(out=squashed[:], in_=fourth[:], func=ACT.Tanh)
-            if not GP:
-                return third, squashed
-            weighted = ring.tile([P, S], F32, name="weighted")
-            nc.gpsimd.tensor_tensor(out=weighted[:], in0=squashed[:], in1=gain2[:], op=ALU.mult)
-            return third, weighted
+            nc.scalar.activation(out=squashed[:], in_=inner[:], func=ACT.Tanh)
+            return plain, squashed
 
-        def combine(slot, pair, op):
-            if pair[0] is None:
-                return pair[1]
-            h = held(slot, [P, S], F32)
-            if pair[1] is None:
-                nc.scalar.copy(out=h[:], in_=pair[0][:])
-            else:
-                nc.vector.tensor_tensor(out=h[:], in0=pair[0][:], in1=pair[1][:], op=op)
-            return h
+        def combine(out, pair, op):
+            nc.vector.tensor_tensor(out=out[:], in0=pair[0][:], in1=pair[1][:], op=op)
+            return out
 
-        def turn_into(sums, rows, first, blocks=range(T2 // P)):
-            for b in blocks:
-                nc.tensor.matmul(
-                    sums[b // 4][:, P * (b % 4) : P * (b % 4 + 1)],
-                    lhsT=rows[:, P * b : P * (b + 1)],
-                    rhs=ident[:],
-                    is_transpose=True,
-                    start=first and b % 4 == 0,
-                    stop=(not first) and b % 4 == 3,
-                )
+        def gate_level(s, h, gate, gated, sums):
+            cols = slice(HALF * h, HALF * (h + 1))
+            nc.vector.tensor_tensor(out=gated[:, cols], in0=level_rows[s][:, cols], in1=gate[:, cols], op=ALU.mult)
+            for b in range(BLOCKS):
+                add_turned(sums[h][:, block(b)], gated[:, block(BLOCKS * h + b)], b == 0, False)
+
+        def add_sinks(page, sums):
+            for h in range(2):
+                for b in range(BLOCKS):
+                    add_turned(sums[h][:, block(b)], page[:, block(BLOCKS * h + b)], False, b == BLOCKS - 1)
 
         z_turned = {}
 
-        def round_z(s, h, sums, copy):
-            if s % 4 == 0:
-                z_turned[s // 4, h] = held("z_turned%d%d" % (s // 4, h), [P, 4 * HALF], BF16)
+        def round_z(s, h, sums, copy, blocks=slice(0, BLOCKS)):
+            a, place = divmod(s, SLICES_A_PASS)
+            if place == 0:
+                z_turned[a, h] = held("z_turned%d%d" % (a, h), [P, PACK * HALF], BF16)
+            whole = z_turned[a, h][:].rearrange("t (b u s q e) -> t b u s q e", u=2, b=BLOCKS, s=SLICES_A_PASS, e=2)
             copy(
-                out=z_turned[s // 4, h][:].rearrange("t (u b s q e) -> t u b s q e", u=2, b=4, s=4, e=2)[
-                    :, :, :, s % 4, :, :
-                ],
-                in_=sums[:].rearrange("t (b q u e) -> t u b q e", b=4, u=2, e=2),
+                out=whole[:, blocks, :, place, :, :],
+                in_=sums[h][:].rearrange("t (b q u e) -> t b u q e", b=BLOCKS, u=2, e=2)[:, blocks],
             )
 
         def turn_back(a, h, banks, copies):
@@ -335,187 +289,163 @@ def tile_list_manhole_source_sink_kernel(
             for k in range(2):
                 turned = bank(banks[k])
                 for u in range(2):
-                    for bb in range(2):
-                        src = (4 * u + 2 * k + bb) * P
-                        dst = (2 * u + bb) * P
-                        nc.tensor.transpose(turned[:, dst : dst + P], words[:, src : src + P], ident[:])
+                    for b in range(2):
+                        nc.tensor.transpose(turned[:, block(2 * u + b)], words[:, block(2 * (2 * k + b) + u)], ident[:])
                 copies[k](
                     out=grouped[:].bitcast(F32)[:, HALF * k : HALF * (k + 1)].rearrange("p (c u) -> p c u", u=2),
                     in_=turned[:].rearrange("p (u c) -> p c u", u=2),
                 )
             return grouped
 
-        def moving(name, grouped, scales=None):
-            codes, scales = quantize(name, grouped, HALF, scales)
-            return codes[:].bitcast(E4M3), scales[:]
-
-        w5_dealt = {}
-
-        def deal_w5(a, tag):
-            w5_dealt[a] = held("w5_dealt%d" % a, [P, PACK, 2 * P], U8, tag=tag)
+        def deal_w5(a, after):
+            dealt = held("w5_dealt%d" % a, [P, PACK, 2 * P], U8, after=after)
             nc.vector.tensor_copy(
-                out=w5_dealt[a][:].bitcast(U16),
-                in_=w5[:, a, :].bitcast(U16).rearrange("p (m t) -> p t m", t=PACK),
+                out=dealt[:].bitcast(U16), in_=w5[:, a, :].bitcast(U16).rearrange("p (m i) -> p i m", i=PACK)
             )
+            return dealt
 
-        def prepare_w6():
-            grouped = held("w6_grouped", [P, PACK * N], BF16, tag="level0")
+        def round_w6():
+            grouped = held("w6_grouped", [P, PACK * N], BF16, after="level0")
             for k in range(2):
+                part = slice(P // 2 * k, P // 2 * (k + 1))
                 nc.scalar.copy(
-                    out=grouped[:].rearrange("p (t m i) -> p m i t", t=PACK, i=PACK)[:, 64 * k : 64 * (k + 1)],
-                    in_=w6_raw[:].rearrange("p i (m t) -> p m i t", t=PACK)[:, 64 * k : 64 * (k + 1)],
+                    out=grouped[:].rearrange("p (i m row) -> p m row i", i=PACK, row=PACK)[:, part],
+                    in_=w6_raw[:].rearrange("p row (m i) -> p m row i", i=PACK)[:, part],
                 )
             return grouped
 
-        def prepare_cells(h):
-            grouped = held("cells_grouped%d" % h, [P, PACK * HALF], BF16, tag="level%d" % (1 + h))
+        def round_cells(h):
+            grouped = held("cells_grouped%d" % h, [P, PACK * HALF], BF16, after="level%d" % (1 + h))
             for k in range(2):
-                round_rows(cells_raw[h], grouped, 256 * k, 256 * (k + 1))
+                c0, c1 = HALF // 2 * k, HALF // 2 * (k + 1)
+                round_rows(grouped[:, PACK * c0 : PACK * c1], cells_raw[h][:, :, c0:c1])
             return grouped
 
-        def w5_slice(a, t):
-            return w5_dealt[a][:, t, :].bitcast(E2M1), w5_plane_dealt[:, a, t, :]
+        quantised = {}
+        pending = []
 
-        z_q, cells_q = {}, {}
-
-        def scatter_sinks(s):
-            nc.vector.tensor_tensor(pages_b[s % PB][:].indirect(list3[:]), sinks[:], gain2[:], ALU.mult)
-
-        page_a = pages_a[0]
-        for s in range(2):
-            round_parts("w1_slice%d" % s, [(w1_raw[0][:, :, P * s : P * (s + 1)], w1_q, s)], "")()
-        sources = {0: combine("features0", source_products(0), ALU.max)}
-        zero_page(pages_b, "page_b0", "tab")
-        if PB == 2:
-            zero_page(pages_b, "page_b1", "w1_raw0")
-        source_pairs = {1: source_products(1)}
-        pending = [round_pair(0)]
-        later = {}
-        gates = {}
-
-        def gate_level(s, halves, gated, sums):
-            for h in halves:
-                cols = slice(HALF * h, HALF * (h + 1))
-                nc.vector.tensor_tensor(out=gated[:, cols], in0=level_sb[s][:, cols], in1=gates[s][:, cols], op=ALU.mult)
-                turn_into(sums, gated, True, range(4 * h, 4 * h + 4))
+        def quantise_later(name, grouped):
+            pending.append(lambda: quantised.setdefault(name, quantize(name, grouped, HALF)))
 
         def finish_pending():
             for finish in pending:
                 finish()
             pending.clear()
 
-        for s in range(SLICES + 1):
-            if s < SLICES:
-                nc.vector.tensor_tensor(page_a[:].indirect(list2[:]), sources[s][:], gain1[:], ALU.mult)
-                gates[s] = ring.tile([P, T2], F32, name="gate", bufs=GATE)
-                nc.scalar.activation(out=gates[s][:], in_=page_a[:], func=ACT.Sigmoid)
-            if s + 1 < SLICES:
-                sources[s + 1] = combine("features%d" % ((s + 1) % NSLOT), source_pairs[s + 1], ALU.max)
-            if QPOS == 0 or s == 0:
-                finish_pending()
-            if s + 2 < SLICES and TPOS == 0:
-                source_pairs[s + 2] = source_products(s + 2)
-            if s > 0:
-                gated = ring.tile([P, T2], F32, name="gated", bufs=GATED)
-                sums = [bank(4), bank(5)]
-                if s == SLICES:
-                    sinks = combine("last_sinks", sink_pair, ALU.mult)
-                    gate_level(s - 1, (0, 1), gated, sums)
-                else:
-                    gate_level(s - 1, (0,), gated, sums)
-                    sinks = combine("features%d" % (s % NSLOT), sink_pair, ALU.mult)
-            if s < SLICES:
-                sink_pair = sink_products(s)
-            if s + 2 < SLICES and TPOS == 1:
-                source_pairs[s + 2] = source_products(s + 2)
-            if 0 < s < SLICES:
-                gate_level(s - 1, (1,), gated, sums)
-            if QPOS == 1:
-                finish_pending()
-            if s == SLICES:
-                break
-            if s in (1, 3, 5):
-                pending.append(round_pair(s // 2 + 1))
-            if s == S_W6:
-                w6_grouped = prepare_w6()
-                pending.append(lambda: later.setdefault("w6", quantize("w6", w6_grouped, N)))
-            if s == S_CELLS:
-                cells_grouped = prepare_cells(0)
-                pending.append(lambda: cells_q.setdefault(0, moving("cells0", cells_grouped)))
-            if s == S_CELLS1:
-                cells_waiting = prepare_cells(1)
-            if s == S_TB0:
-                z_grouped = turn_back(0, 0, (6, 7), (nc.scalar.copy, nc.scalar.copy))
-                pending.append(lambda: z_q.setdefault((0, 0), moving("z00", z_grouped)))
-            if s == S_TB1:
-                z_waiting = turn_back(0, 1, (6, 7), (nc.scalar.copy, nc.scalar.copy))
-            if s > 0:
-                scatter_sinks(s - 1)
-                turn_into(sums, pages_b[(s - 1) % PB], False)
-                for h in range(2):
-                    round_z(s - 1, h, sums[h], nc.scalar.copy)
-            if s == S_DEAL:
-                deal_w5(0, "level3")
-                w5_plane_dealt = held("w5_plane_dealt", [P, 2, PACK, P], U8, tag="level4")
-                nc.vector.tensor_copy(
-                    out=w5_plane_dealt[:], in_=w5_plane[:].rearrange("p a (m t) -> p a t m", t=PACK)
-                )
-        finish_pending()
-        w6_codes, w6_scales = later["w6"]
+        for s in range(2):
+            round_weights("w1_slice%d" % s, [(w1_raw[0][:, :, block(s)], w1_q, s, w1_sign(s))])()
+        first_pair = source_products(0)
+        sources = {0: combine(features(0), first_pair, ALU.max)}
+        source_pairs = {1: source_products(1)}
+        source_page = zero_page(nc.gpsimd, "source_page", after="w1_slice0_codes")
+        sink_pages = [
+            zero_page(nc.gpsimd, "sink_page0", after="w1_slice0_scales"),
+            zero_page(nc.gpsimd, "sink_page1", after="w1_slice1_codes"),
+        ]
+        pending.append(round_pair(0))
+        gates, sink_pairs = {}, {}
 
-        def open_sum(t, h, b):
+        def scatter_sinks(s, sinks):
+            nc.vector.tensor_tensor(sink_pages[s % 2][:].indirect(list3[:]), sinks[:], gain2[:], ALU.mult)
+
+        for s in range(SLICES):
+            page = first_source_page if s == 0 else source_page
+            nc.vector.tensor_tensor(page[:].indirect(list2[:]), sources[s][:], gain1[:], ALU.mult)
+            gates[s] = ring.tile([P, T2], F32, name="gate")
+            nc.scalar.activation(out=gates[s][:], in_=page[:], func=ACT.Sigmoid)
+            if s + 1 in source_pairs:
+                sources[s + 1] = combine(features(s + 1), source_pairs[s + 1], ALU.max)
+            finish_pending()
+            if s > 0:
+                gated = ring.tile([P, T2], F32, name="gated", bufs=1)
+                sums = [bank(4), bank(5)]
+                gate_level(s - 1, 0, gates[s - 1], gated, sums)
+                sinks = combine(features(s), sink_pairs[s - 1], ALU.mult)
+            sink_pairs[s] = sink_products(s)
+            if s + 2 in RELU_SLICES:
+                sources[s + 2] = sources_by_relu(s + 2)
+            elif s + 2 < SLICES:
+                source_pairs[s + 2] = source_products(s + 2)
+            if s > 0:
+                gate_level(s - 1, 1, gates[s - 1], gated, sums)
+            if s % 2 == 1 and s + 1 < SLICES:
+                pending.append(round_pair((s + 1) // 2))
+            if s == CELLS_STEP:
+                quantise_later("cells0", round_cells(0))
+            if s == CELLS_STEP + 1:
+                cells1_grouped = round_cells(1)
+            if s == CELLS_STEP + 2:
+                quantise_later("w6", round_w6())
+            if s == TURN_STEP:
+                quantise_later("z00", turn_back(0, 0, (6, 7), (nc.scalar.copy, nc.scalar.copy)))
+            if s == TURN_STEP + 1:
+                z01_grouped = turn_back(0, 1, (6, 7), (nc.scalar.copy, nc.scalar.copy))
+            if s > 0:
+                scatter_sinks(s - 1, sinks)
+                add_sinks(sink_pages[(s - 1) % 2], sums)
+                for h in range(2):
+                    round_z(s - 1, h, sums, nc.scalar.copy)
+            if s == DEAL_STEP:
+                w5_dealt = [deal_w5(0, after="level3")]
+                w5_plane_dealt = held("w5_plane_dealt", [P, 2, PACK, P], U8, after="level4")
+                nc.vector.tensor_copy(
+                    out=w5_plane_dealt[:], in_=w5_plane[:].rearrange("p a (m i) -> p a i m", i=PACK)
+                )
+
+        last = SLICES - 1
+        gated = held("last_gated", [P, T2], F32, after="level5")
+        sums = [bank(4), bank(5)]
+        gate_level(last, 0, gates[last], gated, sums)
+        sinks = combine(held("last_sinks", [P, S], F32), sink_pairs[last], ALU.mult)
+        gate_level(last, 1, gates[last], gated, sums)
+
+        def w5_set(a, i):
+            return w5_dealt[a][:, i, :].bitcast(E2M1), w5_plane_dealt[:, a, i, :]
+
+        def open_sum(i, h, b):
             acc = bank(b)
-            cols = slice(P * t, P * (t + 1))
-            mx(acc[:], (w6_codes[:, cols].bitcast(E4M3), w6_scales[:, cols]), cells_q[h], True, False)
-            mx(acc[:], w5_slice(0, t), z_q[0, h], False, False)
+            mx(acc[:], columns(quantised["w6"], block(i)), columns(quantised["cells%d" % h]), True, False)
+            mx(acc[:], w5_set(0, i), columns(quantised["z0%d" % h]), False, False)
             return acc
 
-        scatter_sinks(SLICES - 1)
-        page_b = pages_b[(SLICES - 1) % PB]
-        accs = {(t, 0): open_sum(t, 0, t) for t in range(PACK)}
-        turn_into(sums, page_b, False)
-        round_z(SLICES - 1, 0, sums[0], nc.scalar.copy)
-        cells_q[1] = moving("cells1", cells_waiting, held("cells1_scales", [P, HALF], U8, tag="gain2"))
-        deal_w5(1, "level2")
-        z_q[0, 1] = moving("z01", z_waiting, held("z01_scales", [P, HALF], U8, tag="last_sinks"))
-        round_z(SLICES - 1, 1, sums[1], nc.vector.tensor_copy if RZ else nc.scalar.copy)
-        z_q[1, 0] = moving("z10", turn_back(1, 0, (6, 7), (nc.scalar.copy, nc.vector.tensor_copy)))
-        z_q[1, 1] = moving("z11", turn_back(1, 1, (4, 5), (nc.scalar.copy, nc.vector.tensor_copy if WC else nc.scalar.copy)))
-        for t in range(2):
-            accs[t, 1] = open_sum(t, 1, 6 + t)
+        scatter_sinks(last, sinks)
+        accs = {(i, 0): open_sum(i, 0, i) for i in range(PACK)}
+        add_sinks(sink_pages[last % 2], sums)
+        for blocks in (slice(0, 2), slice(2, BLOCKS)):
+            round_z(last, 0, sums, nc.scalar.copy, blocks)
+        quantised["cells1"] = quantize("cells1", cells1_grouped, HALF, scales_after="gain2")
+        w5_dealt.append(deal_w5(1, after="level2"))
+        quantised["z01"] = quantize("z01", z01_grouped, HALF, scales_after="last_sinks")
+        round_z(last, 1, sums, nc.vector.tensor_copy)
+        quantised["z10"] = quantize("z10", turn_back(1, 0, (6, 7), (nc.scalar.copy, nc.vector.tensor_copy)), HALF)
+        quantised["z11"] = quantize("z11", turn_back(1, 1, (4, 5), (nc.scalar.copy, nc.scalar.copy)), HALF)
+        for i in range(2):
+            accs[i, 1] = open_sum(i, 1, 6 + i)
 
-        y_rows = out_0.rearrange("(p t) c -> p t c", t=PACK)
-        y_words = out_1[0].rearrange("p c t -> p (c t)").bitcast(I32)
+        y_rows = out_0.rearrange("(p i) c -> p i c", i=PACK)
+        y_words = out_1[0].rearrange("p c i -> p (c i)").bitcast(I32)
         y_plane = held("y_plane", [P, T2], U8)
-        pieces = 0
         for h in range(2):
-            for t in range(PACK):
-                if h == 1 and t >= 2:
-                    accs[t, 1] = open_sum(t, 1, 2 + t)
-                mx(accs[t, h][:], w5_slice(1, t), z_q[1, h], False, True)
-            cuts = Y_CUTS[h]
-            for c0, c1 in zip(cuts, cuts[1:]):
-                width = c1 - c0
-                cols = slice(HALF * h + c0, HALF * h + c1)
-                y = held("y%d" % pieces, [P, PACK, width], F32, tag="w4_raw%d" % pieces if width <= 256 else "cells_raw%d" % h)
-                for t in range(PACK):
-                    copy = nc.vector.tensor_copy if (VMASK >> (4 * pieces + t)) & 1 else nc.scalar.copy
-                    copy(out=y[:, t, :], in_=accs[t, h][:, c0:c1])
-                    if width == HALF and t % 2 == 1:
-                        nc.sync.dma_start(out=y_rows[:, t - 1 : t + 1, cols], in_=y[:, t - 1 : t + 1, :])
-                if width < HALF:
-                    nc.sync.dma_start(out=y_rows[:, :, cols], in_=y[:])
-                grouped = held("y_grouped%d" % pieces, [P, PACK * width], BF16, tag=("level6", "level7", "w1_raw1", "w1_raw2")[pieces])
-                nc.vector.tensor_copy(
-                    out=grouped[:].rearrange("p (c j t) -> p c t j", j=4, t=PACK),
-                    in_=y[:].rearrange("p t (c j) -> p c t j", j=4),
-                )
-                y_codes = held("y_codes%d" % pieces, [P, width], U32)
-                nc.vector.quantize_mx(out=y_codes[:].bitcast(E4M3), scales=y_plane[:, cols], in_=grouped[:])
-                nc.sync.dma_start(out=y_words[:, cols], in_=y_codes[:].bitcast(I32))
-                pieces = pieces + 1
-        for q in range(4):
+            cols = slice(HALF * h, HALF * (h + 1))
+            for i in range(PACK):
+                if (i, h) not in accs:
+                    accs[i, h] = open_sum(i, h, 2 + i)
+                mx(accs[i, h][:], w5_set(1, i), columns(quantised["z1%d" % h]), False, True)
+            y = held("y%d" % h, [P, PACK, HALF], F32, after="cells_raw%d" % h)
+            for i in range(PACK):
+                copy = nc.vector.tensor_copy if h == 0 and i % 2 == 1 else nc.scalar.copy
+                copy(out=y[:, i, :], in_=accs[i, h][:])
+                nc.sync.dma_start(out=y_rows[:, i : i + 1, cols], in_=y[:, i : i + 1, :])
+            grouped = held("y_grouped%d" % h, [P, PACK * HALF], BF16, after="level%d" % (6 + h))
+            share = SCALAR_SHARE * h
+            out, in_ = interleaved(grouped[:, PACK * share :], y[:, :, share:])
+            nc.vector.tensor_copy(out=out, in_=in_)
+            if share:
+                out, in_ = interleaved(grouped[:, : PACK * share], y[:, :, :share])
+                nc.scalar.copy(out=out, in_=in_)
+            y_codes = held("y_codes%d" % h, [P, HALF], U32)
+            nc.vector.quantize_mx(out=y_codes[:].bitcast(E4M3), scales=y_plane[:, cols], in_=grouped[:])
+            nc.sync.dma_start(out=y_words[:, cols], in_=y_codes[:].bitcast(I32))
+        for q in range(QUADRANTS):
             queue = nc.sync if q % 2 == 0 else nc.scalar
-            queue.dma_start(
-                out=out_2[0, 4 * q : 4 * q + 4, :].bitcast(I32), in_=y_plane[32 * q : 32 * q + 4, :].bitcast(I32)
-            )
+            queue.dma_start(out=out_2[0, 4 * q : 4 * q + 4, :].bitcast(I32), in_=y_plane[live_rows(q), :].bitcast(I32))

@@ -108,10 +108,6 @@ def tile_list_manhole_source_sink_kernel(
             engine.memset(page[:], 0.0)
             return page
 
-        warm = held("warm", [P, 16], F32)
-        nc.vector.memset(warm[:, 0:8], 0.0)
-        nc.scalar.activation(out=warm[:, 8:16], in_=warm[:, 0:8], func=ACT.Sigmoid)
-
         tab_plane = held("tab_plane", [P, T], U8)
         nc.vector.memset(tab_plane[:].bitcast(I32), 0)
         w2_plane = zero_plane("w2_plane", 1, H)
@@ -153,9 +149,9 @@ def tile_list_manhole_source_sink_kernel(
         load_w1(0)
         load(w2[:].bitcast(I32), w2_words[0].bitcast(I32))
         load_plane(w2_plane, w2_scales)
-        load_w4(0)
         nc.sync.dma_start(list2[:], offs2)
         load(gain1[:], wg1)
+        load_w4(0)
         load_w1(1)
         load(w3[:].bitcast(I32), w3_words[0].rearrange("p c i -> p (c i)").bitcast(I32))
         load_plane(w3_plane, w3_scales)

from contextlib import ExitStack

import concourse.mybir as mybir
from concourse.masks import make_identity

K, T, S, T2, H, M, N = 512, 2048, 512, 1024, 1024, 512, 512
FLOPS = 2 * (4 * K * H * S + (H + M) * N * T2)

F32 = mybir.dt.float32
BF16 = mybir.dt.bfloat16
I32 = mybir.dt.int32
U32 = mybir.dt.uint32
U16 = mybir.dt.uint16
U8 = mybir.dt.uint8
E4M3 = mybir.dt.float8_e4m3fn_x4
E2M1 = mybir.dt.float4_e2m1fn_x4
ALU = mybir.AluOpType
ACT = mybir.ActivationFunctionType

P = 128
PACK = 4
QUADRANTS = 4
LINE = 4
SLICES = H // P
SLICES_A_PASS = 4
HALF = 512
BLOCKS = HALF // P
CHUNK = 2 * P

RELU_SLICES = range(2, 7)
FEATURE_TILES = 3
CELLS_STEP = 3
TURN_STEP = SLICES_A_PASS + 1
DEAL_STEP = 6
SCALAR_SHARE = 192


def tile_list_manhole_source_sink_kernel(
    tc, tab_words, tab_scales, offs, offs2, offs3, w1, w2_words, w2_scales, w3_words, w3_scales,
    w4, wg1, wg2, level, w5_words, w5_scales, cells, w6, out_0, out_1, out_2,
):
    nc = tc.nc
    with ExitStack() as ctx:
        keep = ctx.enter_context(tc.tile_pool(name="keep", bufs=1))
        ring = ctx.enter_context(tc.tile_pool(name="ring", bufs=2))
        psum = ctx.enter_context(tc.psum_pool(name="psum", bufs=1))

        def held(name, shape, dtype, after=""):
            return keep.tile(shape, dtype, name=name, tag=after or name, align_bytes=64)

        def bank(b):
            return psum.tile([P, HALF], F32, name="bank%d" % b)

        def load(tile_ap, dram_ap):
            nc.sync.dma_start(out=tile_ap, in_=dram_ap)

        def live_rows(q):
            return slice(32 * q, 32 * q + 4)

        def zero_plane(name, passes, width):
            plane = held(name, [P, passes, width], U8)
            nc.vector.memset(plane[:].rearrange("p a c -> p (a c)").bitcast(I32), 0)
            return plane

        def load_plane(plane, scales):
            for q in range(QUADRANTS):
                rows = scales[:, 4 * q : 4 * q + 4, :].rearrange("a r c -> r a c")
                load(plane[live_rows(q)].bitcast(I32), rows.bitcast(I32))

        def load_rows(name, rows):
            raw = held(name, [P, PACK, rows.shape[1]], F32)
            load(raw[:], rows.rearrange("(p i) c -> p i c", i=PACK))
            return raw

        def interleaved(grouped, raw):
            return (
                grouped.rearrange("p (c j i) -> p c i j", j=LINE, i=PACK),
                raw.rearrange("p i (c j) -> p c i j", j=LINE),
            )

        def round_rows(grouped, raw, sign=1.0):
            out, in_ = interleaved(grouped, raw)
            nc.scalar.activation(out=out, in_=in_, func=ACT.Copy, scale=sign)

        def quantize(name, grouped, width, scales_after=""):
            scales = held(name + "_scales", [P, width], U8, after=scales_after)
            codes = held(name + "_codes", [P, width], U32)
            nc.vector.quantize_mx(out=codes[:].bitcast(E4M3), scales=scales[:], in_=grouped[:])
            return codes, scales

        def columns(operand, cols=slice(None)):
            codes, scales = operand
            return codes[:, cols].bitcast(E4M3), scales[:, cols]

        def mx(out, lhs, rhs, start=True, stop=True):
            nc.tensor.matmul_mx(
                out=out, lhsT=lhs[0], lhsT_scale=lhs[1], rhs=rhs[0], rhs_scale=rhs[1], start=start, stop=stop
            )

        def block(b):
            return slice(P * b, P * (b + 1))

        def add_turned(out, rows, start, stop):
            nc.tensor.matmul(out, lhsT=rows, rhs=ident[:], is_transpose=True, start=start, stop=stop)

        def zero_page(engine, name, after=""):
            page = held(name, [P, T2], F32, after=after)
            engine.memset(page[:], 0.0)
            return page

        tab_plane = held("tab_plane", [P, T], U8)
        nc.vector.memset(tab_plane[:].bitcast(I32), 0)
        w2_plane = zero_plane("w2_plane", 1, H)
        w5_plane = zero_plane("w5_plane", 2, N)
        w3_plane = zero_plane("w3_plane", 1, H)
        first_source_page = zero_page(nc.vector, "first_source_page")
        ident = held("ident", [P, P], F32)
        make_identity(nc, ident[:])

        list1 = held("list1", [P, S // 16], U16)
        list2 = held("list2", [P, S // 16], U16)
        list3 = held("list3", [P, S // 16], U16)
        tab = held("tab", [P, T], U32)
        w2 = held("w2", [P, 2 * H], U8)
        w3 = held("w3", [P, H], U32)
        w5 = held("w5", [P, 2, 2 * N], U8)
        gain1 = held("gain1", [P, S], F32)
        w1_raw, w4_raw, level_rows, cells_raw = [], [], [], []

        def load_w1(c):
            w1_raw.append(load_rows("w1_raw%d" % c, w1[:, CHUNK * c : CHUNK * (c + 1)]))

        def load_w4(c):
            w4_raw.append(load_rows("w4_raw%d" % c, w4[:, CHUNK * c : CHUNK * (c + 1)]))

        def load_level(s):
            rows = held("level%d" % s, [P, T2], F32)
            load(rows[:], level[block(s), :])
            level_rows.append(rows)

        staged = held("staged", [P, T // 4], I32, after="gain2")
        nc.sync.dma_start(list1[:], offs)
        for q in range(QUADRANTS):
            load(staged[live_rows(q), :], tab_scales[0, 4 * q : 4 * q + 4, :].bitcast(I32))
        load(tab[:].bitcast(I32), tab_words[0].rearrange("p t i -> p (t i)").bitcast(I32))
        for q in range(QUADRANTS):
            nc.vector.tensor_copy(out=tab_plane[live_rows(q), :].bitcast(I32), in_=staged[live_rows(q), :])
        gain2 = held("gain2", [P, S], F32)
        load_w1(0)
        load(w2[:].bitcast(I32), w2_words[0].bitcast(I32))
        load_plane(w2_plane, w2_scales)
        nc.sync.dma_start(list2[:], offs2)
        load(gain1[:], wg1)
        load_w4(0)
        load_w1(1)
        load(w3[:].bitcast(I32), w3_words[0].rearrange("p c i -> p (c i)").bitcast(I32))
        load_plane(w3_plane, w3_scales)
        load_level(0)
        nc.sync.dma_start(list3[:], offs3)
        load(gain2[:], wg2)
        load_level(1)
        for c in range(1, H // CHUNK):
            load_w4(c)
            if c + 1 < H // CHUNK:
                load_w1(c + 1)
        for h in range(2):
            load_level(2 + h)
            cells_raw.append(load_rows("cells_raw%d" % h, cells[:, HALF * h : HALF * (h + 1)]))
        load_level(4)
        w6_raw = load_rows("w6_raw", w6)
        load_level(5)
        load(w5[:].bitcast(I32), w5_words.rearrange("a p c -> p a c").bitcast(I32))
        load_plane(w5_plane, w5_scales)
        load_level(6)
        load_level(7)

        v_codes = held("v_codes", [P, S], U32)
        v_scales = held("v_scales", [P, S], U8)
        nc.vector.tensor_copy(v_scales[:], tab_plane[:].indirect(list1[:]))
        nc.vector.tensor_copy(v_codes[:], tab[:].indirect(list1[:]))
        v = (v_codes, v_scales)

        w1_q, w4_q = {}, {}

        def round_weights(name, parts, after=""):
            width = sum(raw.shape[2] for raw, table, first, sign in parts)
            grouped = held(name + "_grouped", [P, PACK * width], BF16, after=after)
            starts = [0]
            for raw, table, first, sign in parts:
                starts.append(starts[-1] + raw.shape[2])
                round_rows(grouped[:, PACK * starts[-2] : PACK * starts[-1]], raw, sign)

            def finish():
                operand = quantize(name, grouped, width)
                for start, (raw, table, first, sign) in zip(starts, parts):
                    for k in range(raw.shape[2] // P):
                        table[first + k] = columns(operand, slice(start + P * k, start + P * (k + 1)))

            return finish

        def w1_sign(s):
            return -1.0 if s in RELU_SLICES else 1.0

        def round_pair(c):
            parts = [(w4_raw[c][:], w4_q, 2 * c, 1.0)]
            if c + 1 < len(w1_raw):
                s = 2 * c + 2
                if w1_sign(s) == w1_sign(s + 1):
                    parts.append((w1_raw[c + 1][:], w1_q, s, w1_sign(s)))
                else:
                    parts.extend((w1_raw[c + 1][:, :, block(k)], w1_q, s + k, w1_sign(s + k)) for k in range(2))
            return round_weights("pair%d" % c, parts, after="first_b")

        def features(turn):
            return held("features%d" % (turn % FEATURE_TILES), [P, S], F32)

        def w2_slice(s):
            return w2[:, 2 * P * s : 2 * P * (s + 1)].bitcast(E2M1), w2_plane[:, 0, block(s)]

        def source_products(s):
            a, b = bank(0), bank(1)
            mx(b[:], w2_slice(s), columns(v))
            mx(a[:], w1_q[s], columns(v))
            b_rows = held("first_b", [P, S], F32) if s == 0 else ring.tile([P, S], F32, name="b_rows")
            nc.scalar.copy(out=b_rows[:], in_=b[:])
            return a, b_rows

        def sources_by_relu(s):
            minus_a, excess = bank(0), bank(1)
            for b in range(BLOCKS):
                v_block = columns(v, block(b))
                mx(excess[:, block(b)], v_block, w2_slice(s), True, False)
                mx(excess[:, block(b)], v_block, w1_q[s], False, True)
                mx(minus_a[:, block(b)], v_block, w1_q[s])
            excess_rows = ring.tile([P, S], F32, name="excess_rows", bufs=1)
            nc.scalar.activation(out=excess_rows[:], in_=excess[:], func=ACT.Relu)
            a_rows = ring.tile([P, S], F32, name="a_rows", bufs=1)
            nc.scalar.activation(out=a_rows[:], in_=minus_a[:], func=ACT.Copy, scale=-1.0)
            larger = bank(6)
            for b in range(BLOCKS):
                add_turned(larger[:, block(b)], excess_rows[:, block(b)], True, False)
                add_turned(larger[:, block(b)], a_rows[:, block(b)], False, True)
            h1 = features(s)
            nc.scalar.copy(out=h1[:], in_=larger[:])
            return h1

        def sink_products(s):
            plain, inner = bank(2), bank(3)
            mx(inner[:], w4_q[s], columns(v))
            mx(plain[:], (w3[:, block(s)].bitcast(E4M3), w3_plane[:, 0, block(s)]), columns(v))
            squashed = ring.tile([P, S], F32, name="squashed")
            nc.scalar.activation(out=squashed[:], in_=inner[:], func=ACT.Tanh)
            return plain, squashed

        def combine(out, pair, op):
            nc.vector.tensor_tensor(out=out[:], in0=pair[0][:], in1=pair[1][:], op=op)
            return out

        def gate_level(s, h, gate, gated, sums):
            cols = slice(HALF * h, HALF * (h + 1))
            nc.vector.tensor_tensor(out=gated[:, cols], in0=level_rows[s][:, cols], in1=gate[:, cols], op=ALU.mult)
            for b in range(BLOCKS):
                add_turned(sums[h][:, block(b)], gated[:, block(BLOCKS * h + b)], b == 0, False)

        def add_sinks(page, sums):
            for h in range(2):
                for b in range(BLOCKS):
                    add_turned(sums[h][:, block(b)], page[:, block(BLOCKS * h + b)], False, b == BLOCKS - 1)

        z_turned = {}

        def round_z(s, h, sums, copy, blocks=slice(0, BLOCKS)):
            a, place = divmod(s, SLICES_A_PASS)
            if place == 0:
                z_turned[a, h] = held("z_turned%d%d" % (a, h), [P, PACK * HALF], BF16)
            whole = z_turned[a, h][:].rearrange("t (b u s q e) -> t b u s q e", u=2, b=BLOCKS, s=SLICES_A_PASS, e=2)
            copy(
                out=whole[:, blocks, :, place, :, :],
                in_=sums[h][:].rearrange("t (b q u e) -> t b u q e", b=BLOCKS, u=2, e=2)[:, blocks],
            )

        def turn_back(a, h, banks, copies):
            words = z_turned[a, h][:].bitcast(F32)
            grouped = ring.tile([P, PACK * HALF], BF16, name="z_grouped", align_bytes=64, bufs=3)
            for k in range(2):
                turned = bank(banks[k])
                for u in range(2):
                    for b in range(2):
                        nc.tensor.transpose(turned[:, block(2 * u + b)], words[:, block(2 * (2 * k + b) + u)], ident[:])
                copies[k](
                    out=grouped[:].bitcast(F32)[:, HALF * k : HALF * (k + 1)].rearrange("p (c u) -> p c u", u=2),
                    in_=turned[:].rearrange("p (u c) -> p c u", u=2),
                )
            return grouped

        def deal_w5(a, after):
            dealt = held("w5_dealt%d" % a, [P, PACK, 2 * P], U8, after=after)
            nc.vector.tensor_copy(
                out=dealt[:].bitcast(U16), in_=w5[:, a, :].bitcast(U16).rearrange("p (m i) -> p i m", i=PACK)
            )
            return dealt

        def round_w6():
            grouped = held("w6_grouped", [P, PACK * N], BF16, after="level0")
            for k in range(2):
                part = slice(P // 2 * k, P // 2 * (k + 1))
                nc.scalar.copy(
                    out=grouped[:].rearrange("p (i m row) -> p m row i", i=PACK, row=PACK)[:, part],
                    in_=w6_raw[:].rearrange("p row (m i) -> p m row i", i=PACK)[:, part],
                )
            return grouped

        def round_cells(h):
            grouped = held("cells_grouped%d" % h, [P, PACK * HALF], BF16, after="level%d" % (1 + h))
            for k in range(2):
                c0, c1 = HALF // 2 * k, HALF // 2 * (k + 1)
                round_rows(grouped[:, PACK * c0 : PACK * c1], cells_raw[h][:, :, c0:c1])
            return grouped

        quantised = {}
        pending = []

        def quantise_later(name, grouped):
            pending.append(lambda: quantised.setdefault(name, quantize(name, grouped, HALF)))

        def finish_pending():
            for finish in pending:
                finish()
            pending.clear()

        for s in range(2):
            round_weights("w1_slice%d" % s, [(w1_raw[0][:, :, block(s)], w1_q, s, w1_sign(s))])()
        first_pair = source_products(0)
        sources = {0: combine(features(0), first_pair, ALU.max)}
        source_pairs = {1: source_products(1)}
        source_page = zero_page(nc.gpsimd, "source_page", after="w1_slice0_codes")
        sink_pages = [
            zero_page(nc.gpsimd, "sink_page0", after="w1_slice0_scales"),
            zero_page(nc.gpsimd, "sink_page1", after="w1_slice1_codes"),
        ]
        pending.append(round_pair(0))
        gates, sink_pairs = {}, {}

        def scatter_sinks(s, sinks):
            nc.vector.tensor_tensor(sink_pages[s % 2][:].indirect(list3[:]), sinks[:], gain2[:], ALU.mult)

        for s in range(SLICES):
            page = first_source_page if s == 0 else source_page
            nc.vector.tensor_tensor(page[:].indirect(list2[:]), sources[s][:], gain1[:], ALU.mult)
            gates[s] = ring.tile([P, T2], F32, name="gate")
            nc.scalar.activation(out=gates[s][:], in_=page[:], func=ACT.Sigmoid)
            if s + 1 in source_pairs:
                sources[s + 1] = combine(features(s + 1), source_pairs[s + 1], ALU.max)
            finish_pending()
            if s > 0:
                gated = ring.tile([P, T2], F32, name="gated", bufs=1)
                sums = [bank(4), bank(5)]
                gate_level(s - 1, 0, gates[s - 1], gated, sums)
                sinks = combine(features(s), sink_pairs[s - 1], ALU.mult)
            sink_pairs[s] = sink_products(s)
            if s + 2 in RELU_SLICES:
                sources[s + 2] = sources_by_relu(s + 2)
            elif s + 2 < SLICES:
                source_pairs[s + 2] = source_products(s + 2)
            if s > 0:
                gate_level(s - 1, 1, gates[s - 1], gated, sums)
            if s % 2 == 1 and s + 1 < SLICES:
                pending.append(round_pair((s + 1) // 2))
            if s == CELLS_STEP:
                quantise_later("cells0", round_cells(0))
            if s == CELLS_STEP + 1:
                cells1_grouped = round_cells(1)
            if s == CELLS_STEP + 2:
                quantise_later("w6", round_w6())
            if s == TURN_STEP:
                quantise_later("z00", turn_back(0, 0, (6, 7), (nc.scalar.copy, nc.scalar.copy)))
            if s == TURN_STEP + 1:
                z01_grouped = turn_back(0, 1, (6, 7), (nc.scalar.copy, nc.scalar.copy))
            if s > 0:
                scatter_sinks(s - 1, sinks)
                add_sinks(sink_pages[(s - 1) % 2], sums)
                for h in range(2):
                    round_z(s - 1, h, sums, nc.scalar.copy)
            if s == DEAL_STEP:
                w5_dealt = [deal_w5(0, after="level3")]
                w5_plane_dealt = held("w5_plane_dealt", [P, 2, PACK, P], U8, after="level4")
                nc.vector.tensor_copy(
                    out=w5_plane_dealt[:], in_=w5_plane[:].rearrange("p a (m i) -> p a i m", i=PACK)
                )

        last = SLICES - 1
        gated = held("last_gated", [P, T2], F32, after="level5")
        sums = [bank(4), bank(5)]
        gate_level(last, 0, gates[last], gated, sums)
        sinks = combine(held("last_sinks", [P, S], F32), sink_pairs[last], ALU.mult)
        gate_level(last, 1, gates[last], gated, sums)

        def w5_set(a, i):
            return w5_dealt[a][:, i, :].bitcast(E2M1), w5_plane_dealt[:, a, i, :]

        def open_sum(i, h, b):
            acc = bank(b)
            mx(acc[:], columns(quantised["w6"], block(i)), columns(quantised["cells%d" % h]), True, False)
            mx(acc[:], w5_set(0, i), columns(quantised["z0%d" % h]), False, False)
            return acc

        scatter_sinks(last, sinks)
        accs = {(i, 0): open_sum(i, 0, i) for i in range(PACK)}
        add_sinks(sink_pages[last % 2], sums)
        for blocks in (slice(0, 2), slice(2, BLOCKS)):
            round_z(last, 0, sums, nc.scalar.copy, blocks)
        quantised["cells1"] = quantize("cells1", cells1_grouped, HALF, scales_after="gain2")
        w5_dealt.append(deal_w5(1, after="level2"))
        quantised["z01"] = quantize("z01", z01_grouped, HALF, scales_after="last_sinks")
        round_z(last, 1, sums, nc.vector.tensor_copy)
        quantised["z10"] = quantize("z10", turn_back(1, 0, (6, 7), (nc.scalar.copy, nc.vector.tensor_copy)), HALF)
        quantised["z11"] = quantize("z11", turn_back(1, 1, (4, 5), (nc.scalar.copy, nc.scalar.copy)), HALF)
        for i in range(2):
            accs[i, 1] = open_sum(i, 1, 6 + i)

        y_rows = out_0.rearrange("(p i) c -> p i c", i=PACK)
        y_words = out_1[0].rearrange("p c i -> p (c i)").bitcast(I32)
        y_plane = held("y_plane", [P, T2], U8)
        for h in range(2):
            cols = slice(HALF * h, HALF * (h + 1))
            for i in range(PACK):
                if (i, h) not in accs:
                    accs[i, h] = open_sum(i, h, 2 + i)
                mx(accs[i, h][:], w5_set(1, i), columns(quantised["z1%d" % h]), False, True)
            y = held("y%d" % h, [P, PACK, HALF], F32, after="cells_raw%d" % h)
            for i in range(PACK):
                copy = nc.vector.tensor_copy if h == 0 and i % 2 == 1 else nc.scalar.copy
                copy(out=y[:, i, :], in_=accs[i, h][:])
                nc.sync.dma_start(out=y_rows[:, i : i + 1, cols], in_=y[:, i : i + 1, :])
            grouped = held("y_grouped%d" % h, [P, PACK * HALF], BF16, after="level%d" % (6 + h))
            share = SCALAR_SHARE * h
            out, in_ = interleaved(grouped[:, PACK * share :], y[:, :, share:])
            nc.vector.tensor_copy(out=out, in_=in_)
            if share:
                out, in_ = interleaved(grouped[:, : PACK * share], y[:, :, :share])
                nc.scalar.copy(out=out, in_=in_)
            y_codes = held("y_codes%d" % h, [P, HALF], U32)
            nc.vector.quantize_mx(out=y_codes[:].bitcast(E4M3), scales=y_plane[:, cols], in_=grouped[:])
            nc.sync.dma_start(out=y_words[:, cols], in_=y_codes[:].bitcast(I32))
        for q in range(QUADRANTS):
            queue = nc.sync if q % 2 == 0 else nc.scalar
            queue.dma_start(out=out_2[0, 4 * q : 4 * q + 4, :].bitcast(I32), in_=y_plane[live_rows(q), :].bitcast(I32))
